import numpy as np
import ml_dtypes


def mxq(x, axis, fmt="e4m3"):
    dtype, down = {"e4m3": (ml_dtypes.float8_e4m3fn, 7), "e5m2": (ml_dtypes.float8_e5m2, 14)}[fmt]
    v = np.moveaxis(np.asarray(x, np.float32).astype(ml_dtypes.bfloat16).astype(np.float64), axis, -1)
    blocks = v.reshape(v.shape[:-1] + (-1, 32))
    amax = np.abs(blocks).max(-1, keepdims=True)
    byte = np.maximum(np.where(amax > 0, np.frexp(amax)[1] - 1 + 127, 0) - down, 1)
    scale = np.exp2(byte - 127.0)
    codes = (blocks / scale).astype(np.float32).astype(dtype).astype(np.float64)
    return np.moveaxis((codes * scale).reshape(v.shape), -1, axis)


WIDE = False


def mx_kscale(k):
    if not WIDE:
        return np.ones(k)
    levels = np.array([10, -10, 5, -5, 0])
    if k % 512:
        return np.exp2(np.random.permutation(np.resize(levels, k // 32))).repeat(32)
    a = np.empty((k // 512, 16))
    for p in range(k // 512):
        a[p, :8] = np.random.permutation(np.resize(levels, 8))
        for g in range(8):
            far = levels[np.abs(levels - a[p, g]) >= 10]
            a[p, g + 8] = far[np.random.randint(len(far))]
    return np.exp2(a.ravel()).repeat(32)


def f64(x):
    return np.asarray(x).astype(np.float64)


def striped(idx):
    return np.tile(idx.reshape(-1, 16).T, (8, 1)).astype(np.uint16)


def unstriped(offs):
    return offs[:16].T.reshape(-1).astype(np.int64)


def striped8(idx):
    return np.concatenate([x.reshape(-1, 16).T for x in idx]).astype(np.uint16)


def runs(offs, k):
    lists = np.stack([offs[16 * r : 16 * r + 16].T.reshape(-1) for r in range(8)]).astype(np.int64)
    return lists[np.arange(k) % 512 // 64]


def pack_weight(w):
    k, n = w.shape
    w = f64(np.asarray(w, np.float32).astype(ml_dtypes.bfloat16)).reshape(k // 32, 32, n)
    amax = np.abs(w).max(1)
    byte = np.clip(np.where(amax > 0, np.frexp(amax)[1] - 1 + 127 - 7, 1), 1, 254)
    scaled = (w * np.exp2(127.0 - byte)[:, None, :]).reshape(k, n).astype(np.float32)
    words = np.ascontiguousarray(scaled.reshape(k // 512, 128, 4, n).transpose(0, 1, 3, 2)).astype(ml_dtypes.float8_e4m3fn).view(np.uint8)
    return words, np.ascontiguousarray(byte.astype(np.uint8).reshape(k // 512, 16, n))


def unpack_weight(words, scales):
    g, p, n, _ = words.shape
    vals = np.ascontiguousarray(words).view(ml_dtypes.float8_e4m3fn).astype(np.float64) * np.repeat(np.exp2(scales.astype(np.float64) - 127.0), 8, axis=1)[..., None]
    return vals.transpose(0, 1, 3, 2).reshape(g * 512, n)


def silu(v):
    return v / (1.0 + np.exp(-np.maximum(v, -700.0)))

def planes(y):
    n, m = y.shape
    v = y.astype(np.float32).astype(ml_dtypes.bfloat16).astype(np.float64).reshape(n // 32, 32, m)
    top = np.abs(v).max(1)
    byte = np.clip(np.where(top > 0, np.frexp(top)[1] - 1 + 127 - 7, 1), 1, 254)
    codes = (v * np.exp2(127.0 - byte)[:, None, :]).reshape(n, m).astype(np.float32).astype(ml_dtypes.float8_e4m3fn).view(np.uint8)
    words = codes.reshape(n // 512, 128, 4, m).transpose(0, 1, 3, 2)
    return np.ascontiguousarray(words), np.ascontiguousarray(byte.astype(np.uint8).reshape(n // 512, 16, m))


K, T, S, V, N, H = 512, 2048, 512, 256, 512, 512


def setup_inputs():
    n = np.random.standard_normal
    s = mx_kscale(K)[:, None]
    u = mx_kscale(H)
    packed_xT = pack_weight(n((K, T)) * s)
    packed_w2 = pack_weight(n((H, N)) / np.sqrt(H) / u[:, None])
    return {
        "x_words": packed_xT[0],
        "x_scales": packed_xT[1],
        "w1": (n((K, H)) / np.sqrt(K) / s * u).astype(np.float32),
        "sg1": np.sign(n((H, V))).astype(np.float32),
        "sg2": np.sign(n((H, V))).astype(np.float32),
        "sg3": np.sign(n((H, V))).astype(np.float32),
        "w2_words": packed_w2[0],
        "w2_scales": packed_w2[1],
        "offs": striped(np.random.permutation(T)[:S]),
        "h1": striped8(np.stack([np.random.permutation(S)[:V] for _ in range(8)])),
        "h2": striped8(np.stack([np.random.permutation(S)[:V] for _ in range(8)])),
        "h3": striped8(np.stack([np.random.permutation(S)[:V] for _ in range(8)])),
    }


def reference(x_words, x_scales, w1, sg1, sg2, sg3, w2_words, w2_scales, offs, h1, h2, h3):
    xq = unpack_weight(x_words, x_scales)[:, unstriped(offs)]
    y = mxq(f64(w1), 0, "e4m3").T @ xq
    t1 = f64(sg1) * (y[np.arange(H)[:, None], runs(h1, H)])
    t2 = f64(sg2) * (y[np.arange(H)[:, None], runs(h2, H)])
    t3 = f64(sg3) * (y[np.arange(H)[:, None], runs(h3, H)])
    z = silu(np.maximum(np.minimum(t1, t2), np.minimum(np.maximum(t1, t2), t3)))
    out_0 = unpack_weight(w2_words, w2_scales).T @ mxq(z, 0, "e4m3")
    return (out_0,) + planes(out_0)

@@ -1,0 +1,249 @@
+from contextlib import ExitStack
+
+import concourse.mybir as mybir
+
+K, T, S, V, N, H = 512, 2048, 512, 256, 512, 512
+FLOPS = 2 * K * H * S + 2 * H * N * V
+
+F32 = mybir.dt.float32
+BF16 = mybir.dt.bfloat16
+I32 = mybir.dt.int32
+U32 = mybir.dt.uint32
+U16 = mybir.dt.uint16
+U8 = mybir.dt.uint8
+FP8X4 = mybir.dt.float8_e4m3fn_x4
+ALU = mybir.AluOpType
+SILU = mybir.ActivationFunctionType.Silu
+
+P = 128
+PACK = 4
+QUADS = 4
+HALF = V // 2
+W1_VECTOR_M = 48
+
+
+def tile_picked_csketch_silu_po_kernel(
+    tc, x_words, x_scales, w1, sg1, sg2, sg3, w2_words, w2_scales, offs, h1, h2, h3, out_0, out_1, out_2
+):
+    nc = tc.nc
+    with ExitStack() as ctx:
+        lists = ctx.enter_context(tc.tile_pool(name="lists", bufs=1))
+        keep = ctx.enter_context(tc.tile_pool(name="keep", bufs=1))
+        psum = ctx.enter_context(tc.psum_pool(name="psum", bufs=1))
+
+        def sb(name, cols, dtype):
+            return keep.tile([P, cols], dtype, name=name, align_bytes=64)
+
+        offs_sb = lists.tile([P, S // 16], U16, name="offs_sb")
+        hash_sb = [lists.tile([P, V // 16], U16, name="hash%d" % n) for n in range(3)]
+
+        x_scale_table = sb("x_scale_table", T, U8)
+        nc.gpsimd.memset(x_scale_table[:, : T // 2].bitcast(I32), 0)
+        nc.vector.memset(x_scale_table[:, T // 2 :].bitcast(I32), 0)
+        warm_in = sb("warm_in", 8, F32)
+        warm_out = sb("warm_out", 8, F32)
+        nc.vector.memset(warm_in[:], 0.0)
+        nc.scalar.activation(warm_out[:], warm_in[:], SILU)
+
+        nc.sync.dma_start(offs_sb[:], offs)
+        w1_raw = keep.tile([P, PACK * H], F32, name="w1_raw", align_bytes=64)
+        nc.sync.dma_start(w1_raw[:], w1.rearrange("(p j) c -> p (j c)", j=PACK))
+        for q in range(QUADS):
+            nc.sync.dma_start(
+                x_scale_table[32 * q : 32 * q + 4, :].bitcast(I32), x_scales[0, 4 * q : 4 * q + 4, :].bitcast(I32)
+            )
+        x_word_table = sb("x_word_table", T, I32)
+        nc.sync.dma_start(x_word_table[:], x_words[0].rearrange("p c r -> p (c r)").bitcast(I32))
+        w2_word_raw = keep.tile([P, N], I32, name="w2_word_raw", tag="w2_moved", align_bytes=64)
+        nc.sync.dma_start(w2_word_raw[:], w2_words[0].rearrange("p c r -> p (c r)").bitcast(I32))
+
+        for tile, h in zip(hash_sb, (h1, h2, h3)):
+            nc.sync.dma_start(tile[:], h)
+        w2_scale_raw = sb("w2_scale_raw", N, U8)
+        nc.gpsimd.memset(w2_scale_raw[:].bitcast(I32), 0)
+        signs = {}
+        for pair in range(2):
+            for n, sg in enumerate((sg1, sg2, sg3)):
+                signs[n, pair] = sb("sign%d_%d" % (n, pair), 2 * V, F32)
+                rows = sg.rearrange("(p t) v -> p (t v)", t=PACK)
+                nc.sync.dma_start(signs[n, pair][:], rows[:, 2 * V * pair : 2 * V * (pair + 1)])
+        for q in range(QUADS):
+            nc.gpsimd.dma_start(
+                w2_scale_raw[32 * q : 32 * q + 4, :].bitcast(I32), w2_scales[0, 4 * q : 4 * q + 4, :].bitcast(I32)
+            )
+
+        w1_bf = sb("w1_bf", PACK * H, BF16)
+        w1_dst = w1_bf[:].rearrange("p (t m j) -> p m t j", t=PACK, j=PACK)
+        w1_src = w1_raw[:].rearrange("p (j m t) -> p m t j", t=PACK, j=PACK)
+        nc.vector.tensor_copy(w1_dst[:, :W1_VECTOR_M], w1_src[:, :W1_VECTOR_M])
+        nc.scalar.copy(w1_dst[:, W1_VECTOR_M:], w1_src[:, W1_VECTOR_M:])
+        x_scale = sb("x_scale", S, U8)
+        nc.vector.tensor_copy(x_scale[:], x_scale_table[:].indirect(offs_sb[:]))
+        w1_code = sb("w1_code", H, U32)
+        w1_scale = sb("w1_scale", H, U8)
+        nc.vector.quantize_mx(out=w1_code[:].bitcast(FP8X4), scales=w1_scale[:], in_=w1_bf[:])
+
+        x_word = [sb("x_word%d" % a, S // 2, U32) for a in range(2)]
+        for a in range(2):
+            nc.vector.tensor_copy(
+                x_word[a][:], x_word_table[:].bitcast(U32).indirect(offs_sb[:, a * 16 : (a + 1) * 16])
+            )
+
+        y = [sb("y%d" % t, S, F32) for t in range(PACK)]
+
+        def first(acc, t, a):
+            rows = slice(t * P, (t + 1) * P)
+            nc.tensor.matmul_mx(
+                out=acc,
+                lhsT=w1_code[:, rows].bitcast(FP8X4),
+                lhsT_scale=w1_scale[:, rows],
+                rhs=x_word[a][:].bitcast(FP8X4),
+                rhs_scale=x_scale[:, a * 256 : (a + 1) * 256],
+                start=True,
+                stop=True,
+            )
+
+        for a in range(2):
+            acc = psum.tile([P, S // 2], F32, name="y_acc0_%d" % a)
+            first(acc[:], 0, a)
+            nc.scalar.copy(y[0][:, a * 256 : (a + 1) * 256], acc[:])
+        for t in range(1, PACK):
+            acc = psum.tile([P, S], F32, name="y_acc%d" % t)
+            for a in range(2):
+                first(acc[:, a * 256 : (a + 1) * 256], t, a)
+            nc.scalar.copy(y[t][:], acc[:])
+
+        w2_word = sb("w2_word", N, I32)
+        nc.vector.tensor_copy(
+            w2_word[:].rearrange("p (t c i) -> p c t i", t=PACK, i=4),
+            w2_word_raw[:].rearrange("p (c i t) -> p c t i", t=PACK, i=4),
+        )
+        w2_scale = keep.tile([P, N], U8, name="w2_scale", tag="w2_moved", align_bytes=64)
+        nc.vector.tensor_copy(
+            w2_scale[:].rearrange("p (t c i) -> p c t i", t=PACK, i=16),
+            w2_scale_raw[:].rearrange("p (c i t) -> p c t i", t=PACK, i=16),
+        )
+
+        def plane(tile, t0, t1):
+            return tile[:, t0 * HALF : t1 * HALF]
+
+        looked = {(n, h): sb("looked%d_%d" % (n, h), PACK * HALF, F32) for n in range(3) for h in range(2) if (n, h) != (1, 1)}
+        lo = [sb("lo%d" % h, PACK * HALF, F32) for h in range(2)]
+        hi = [sb("hi%d" % h, PACK * HALF, F32) for h in range(2)]
+        capped = [sb("capped%d" % h, PACK * HALF, F32) for h in range(2)]
+        median = [sb("median%d" % h, PACK * HALF, F32) for h in range(2)]
+        z_bf = [keep.tile([P, PACK * HALF], BF16, name="z_bf0", tag="reused", align_bytes=64), sb("z_bf1", PACK * HALF, BF16)]
+        z_code = [sb("z_code%d" % h, HALF, U32) for h in range(2)]
+        z_scale = [sb("z_scale%d" % h, HALF, U8) for h in range(2)]
+        res = [sb("res%d" % h, PACK * HALF, F32) for h in range(2)]
+        res_bf = [sb("res_bf%d" % h, PACK * HALF, BF16) for h in range(2)]
+        res_code = sb("res_code", V, U32)
+        res_scale = sb("res_scale", V, U8)
+        out_rows = out_0.rearrange("(p t) v -> p t v", t=PACK)
+        out_words = out_1[0].rearrange("p c r -> p (c r)").bitcast(I32)
+
+        def look(n, h, t):
+            sign = signs[n, t // 2][:, (t % 2) * V + h * HALF : (t % 2) * V + (h + 1) * HALF]
+            offsets = hash_sb[n][:, h * HALF // 16 : (h + 1) * HALF // 16]
+            nc.vector.tensor_tensor(plane(looked[n, h], t, t + 1), y[t][:].indirect(offsets), sign, ALU.mult)
+
+        def low(h):
+            nc.vector.tensor_tensor(lo[h][:], looked[0, h][:], looked[1, h][:], ALU.min)
+
+        def high(h):
+            nc.vector.tensor_tensor(hi[h][:], looked[0, h][:], looked[1, h][:], ALU.max)
+
+        def cap(h, t0, t1):
+            nc.vector.tensor_tensor(plane(capped[h], t0, t1), plane(hi[h], t0, t1), plane(looked[2, h], t0, t1), ALU.min)
+
+        def mid(h, t0, t1):
+            nc.vector.tensor_tensor(plane(median[h], t0, t1), plane(lo[h], t0, t1), plane(capped[h], t0, t1), ALU.max)
+
+        def woven(tile, t0, t1):
+            return tile[:].rearrange("p (c i t) -> p c t i", t=PACK, i=4)[:, :, t0:t1, :]
+
+        def planes(ap, count):
+            return ap.rearrange("p (t c i) -> p c t i", t=count, i=4)
+
+        def silu(h, t0, t1):
+            nc.scalar.activation(woven(z_bf[h], t0, t1), planes(plane(median[h], t0, t1), t1 - t0), SILU)
+
+        def quantise_z(h):
+            nc.vector.quantize_mx(out=z_code[h][:].bitcast(FP8X4), scales=z_scale[h][:], in_=z_bf[h][:])
+
+        def second(h, t0, t1):
+            acc = psum.tile([P, (t1 - t0) * HALF], F32, name="out_acc%d_%d" % (h, t0))
+            for t in range(t0, t1):
+                rows = slice(t * P, (t + 1) * P)
+                nc.tensor.matmul_mx(
+                    out=acc[:, (t - t0) * HALF : (t - t0 + 1) * HALF],
+                    lhsT=w2_word[:, rows].bitcast(FP8X4),
+                    lhsT_scale=w2_scale[:, rows],
+                    rhs=z_code[h][:].bitcast(FP8X4),
+                    rhs_scale=z_scale[h][:],
+                    start=True,
+                    stop=True,
+                )
+            return acc
+
+        def store_rows(h, t0, t1):
+            nc.sync.dma_start(
+                out_rows[:, t0:t1, h * HALF : (h + 1) * HALF],
+                plane(res[h], t0, t1).rearrange("p (t v) -> p t v", v=HALF),
+            )
+
+        def quantise_res(h):
+            cols = slice(h * HALF, (h + 1) * HALF)
+            nc.vector.quantize_mx(out=res_code[:, cols].bitcast(FP8X4), scales=res_scale[:, cols], in_=res_bf[h][:])
+            nc.sync.dma_start(out_words[:, cols], res_code[:, cols].bitcast(I32))
+
+        for t in range(PACK):
+            for n in range(3):
+                look(n, 0, t)
+        low(0)
+        high(0)
+        look(0, 1, 0)
+        cap(0, 0, PACK)
+        look(0, 1, 1)
+        mid(0, 0, PACK)
+        silu(0, 0, PACK)
+        look(0, 1, 2)
+        look(0, 1, 3)
+        quantise_z(0)
+        looked[1, 1] = keep.tile([P, PACK * HALF], F32, name="looked1_1", tag="reused", align_bytes=64)
+        look(1, 1, 0)
+        acc = second(0, 0, PACK)
+        nc.scalar.copy(res[0][:], acc[:])
+        store_rows(0, 0, PACK)
+        nc.scalar.copy(woven(res_bf[0], 0, PACK), planes(res[0][:], PACK))
+        look(1, 1, 1)
+        look(1, 1, 2)
+        look(1, 1, 3)
+        look(2, 1, 0)
+        low(1)
+        high(1)
+        look(2, 1, 1)
+        look(2, 1, 2)
+        cap(1, 0, 3)
+        look(2, 1, 3)
+        mid(1, 0, 3)
+        silu(1, 0, 3)
+        cap(1, 3, 4)
+        quantise_res(0)
+        mid(1, 3, 4)
+        silu(1, 3, 4)
+        quantise_z(1)
+        acc_a = second(1, 0, 2)
+        acc_b = second(1, 2, 4)
+        nc.scalar.copy(plane(res[1], 0, 2), acc_a[:])
+        store_rows(1, 0, 2)
+        nc.vector.tensor_copy(woven(res_bf[1], 2, 4), planes(acc_b[:], 2))
+        nc.scalar.copy(plane(res[1], 2, 4), acc_b[:])
+        store_rows(1, 2, 4)
+        nc.vector.tensor_copy(woven(res_bf[1], 0, 2), planes(plane(res[1], 0, 2), 2))
+        quantise_res(1)
+        for q in range(QUADS):
+            queue = nc.sync if q < 2 else nc.scalar
+            queue.dma_start(
+                out_2[0, 4 * q : 4 * q + 4, :].bitcast(I32), res_scale[32 * q : 32 * q + 4, :].bitcast(I32)
+            )

@@ -19,7 +19,6 @@ P = 128
 PACK = 4
 QUADS = 4
 HALF = V // 2
-W1_VECTOR_M = 48
 
 
 def tile_picked_csketch_silu_po_kernel(
@@ -52,36 +51,35 @@ def tile_picked_csketch_silu_po_kernel(
             nc.sync.dma_start(
                 x_scale_table[32 * q : 32 * q + 4, :].bitcast(I32), x_scales[0, 4 * q : 4 * q + 4, :].bitcast(I32)
             )
-        x_word_table = sb("x_word_table", T, I32)
+        x_word_table = keep.tile([P, T], I32, name="x_word_table", tag="x_words_then_w1", align_bytes=64)
         nc.sync.dma_start(x_word_table[:], x_words[0].rearrange("p c r -> p (c r)").bitcast(I32))
-        w2_word_raw = keep.tile([P, N], I32, name="w2_word_raw", tag="w2_moved", align_bytes=64)
+        w2_word_raw = sb("w2_word_raw", N, I32)
         nc.sync.dma_start(w2_word_raw[:], w2_words[0].rearrange("p c r -> p (c r)").bitcast(I32))
 
         for tile, h in zip(hash_sb, (h1, h2, h3)):
             nc.sync.dma_start(tile[:], h)
         w2_scale_raw = sb("w2_scale_raw", N, U8)
         nc.gpsimd.memset(w2_scale_raw[:].bitcast(I32), 0)
-        signs = {}
-        for pair in range(2):
-            for n, sg in enumerate((sg1, sg2, sg3)):
-                signs[n, pair] = sb("sign%d_%d" % (n, pair), 2 * V, F32)
-                rows = sg.rearrange("(p t) v -> p (t v)", t=PACK)
-                nc.sync.dma_start(signs[n, pair][:], rows[:, 2 * V * pair : 2 * V * (pair + 1)])
+        signs = [
+            keep.tile([P, PACK * V], F32, name="sign%d" % n, tag="sign%d" % n, align_bytes=64) for n in range(3)
+        ]
+        for tile, sg in zip(signs, (sg1, sg2, sg3)):
+            nc.sync.dma_start(tile[:], sg.rearrange("(p t) v -> p (t v)", t=PACK))
         for q in range(QUADS):
-            nc.gpsimd.dma_start(
+            nc.sync.dma_start(
                 w2_scale_raw[32 * q : 32 * q + 4, :].bitcast(I32), w2_scales[0, 4 * q : 4 * q + 4, :].bitcast(I32)
             )
 
-        w1_bf = sb("w1_bf", PACK * H, BF16)
-        w1_dst = w1_bf[:].rearrange("p (t m j) -> p m t j", t=PACK, j=PACK)
         w1_src = w1_raw[:].rearrange("p (j m t) -> p m t j", t=PACK, j=PACK)
-        nc.vector.tensor_copy(w1_dst[:, :W1_VECTOR_M], w1_src[:, :W1_VECTOR_M])
-        nc.scalar.copy(w1_dst[:, W1_VECTOR_M:], w1_src[:, W1_VECTOR_M:])
+        w1_bf = [sb("w1_bf%d" % a, 2 * H, BF16) for a in range(2)]
+        w1_code = [sb("w1_code0", 2 * P, U32)]
+        w1_scale = [sb("w1_scale%d" % a, 2 * P, U8) for a in range(2)]
+        w1_dst = [tile[:].rearrange("p (t m j) -> p m t j", t=2, j=PACK) for tile in w1_bf]
+        nc.vector.tensor_copy(w1_dst[0], w1_src[:, :, 0:2, :])
+        nc.scalar.copy(w1_dst[1], w1_src[:, :, 2:4, :])
         x_scale = sb("x_scale", S, U8)
         nc.vector.tensor_copy(x_scale[:], x_scale_table[:].indirect(offs_sb[:]))
-        w1_code = sb("w1_code", H, U32)
-        w1_scale = sb("w1_scale", H, U8)
-        nc.vector.quantize_mx(out=w1_code[:].bitcast(FP8X4), scales=w1_scale[:], in_=w1_bf[:])
+        nc.vector.quantize_mx(out=w1_code[0][:].bitcast(FP8X4), scales=w1_scale[0][:], in_=w1_bf[0][:])
 
         x_word = [sb("x_word%d" % a, S // 2, U32) for a in range(2)]
         for a in range(2):
@@ -89,14 +87,16 @@ def tile_picked_csketch_silu_po_kernel(
                 x_word[a][:], x_word_table[:].bitcast(U32).indirect(offs_sb[:, a * 16 : (a + 1) * 16])
             )
 
+        w1_code.append(keep.tile([P, 2 * P], U32, name="w1_code1", tag="x_words_then_w1", align_bytes=64))
+        nc.vector.quantize_mx(out=w1_code[1][:].bitcast(FP8X4), scales=w1_scale[1][:], in_=w1_bf[1][:])
         y = [sb("y%d" % t, S, F32) for t in range(PACK)]
 
         def first(acc, t, a):
-            rows = slice(t * P, (t + 1) * P)
+            rows = slice(t % 2 * P, (t % 2 + 1) * P)
             nc.tensor.matmul_mx(
                 out=acc,
-                lhsT=w1_code[:, rows].bitcast(FP8X4),
-                lhsT_scale=w1_scale[:, rows],
+                lhsT=w1_code[t // 2][:, rows].bitcast(FP8X4),
+                lhsT_scale=w1_scale[t // 2][:, rows],
                 rhs=x_word[a][:].bitcast(FP8X4),
                 rhs_scale=x_scale[:, a * 256 : (a + 1) * 256],
                 start=True,
@@ -118,21 +118,19 @@ def tile_picked_csketch_silu_po_kernel(
             w2_word[:].rearrange("p (t c i) -> p c t i", t=PACK, i=4),
             w2_word_raw[:].rearrange("p (c i t) -> p c t i", t=PACK, i=4),
         )
-        w2_scale = keep.tile([P, N], U8, name="w2_scale", tag="w2_moved", align_bytes=64)
-        nc.vector.tensor_copy(
-            w2_scale[:].rearrange("p (t c i) -> p c t i", t=PACK, i=16),
-            w2_scale_raw[:].rearrange("p (c i t) -> p c t i", t=PACK, i=16),
-        )
-
         def plane(tile, t0, t1):
             return tile[:, t0 * HALF : t1 * HALF]
 
-        looked = {(n, h): sb("looked%d_%d" % (n, h), PACK * HALF, F32) for n in range(3) for h in range(2) if (n, h) != (1, 1)}
+        pair = [sb("pair%d" % n, PACK * V, F32) for n in range(2)]
         lo = [sb("lo%d" % h, PACK * HALF, F32) for h in range(2)]
         hi = [sb("hi%d" % h, PACK * HALF, F32) for h in range(2)]
+        third = [sb("third0", PACK * HALF, F32)]
         capped = [sb("capped%d" % h, PACK * HALF, F32) for h in range(2)]
         median = [sb("median%d" % h, PACK * HALF, F32) for h in range(2)]
-        z_bf = [keep.tile([P, PACK * HALF], BF16, name="z_bf0", tag="reused", align_bytes=64), sb("z_bf1", PACK * HALF, BF16)]
+        z_bf = [
+            keep.tile([P, PACK * HALF], BF16, name="z_bf0", tag="z_then_third", align_bytes=64),
+            sb("z_bf1", PACK * HALF, BF16),
+        ]
         z_code = [sb("z_code%d" % h, HALF, U32) for h in range(2)]
         z_scale = [sb("z_scale%d" % h, HALF, U8) for h in range(2)]
         res = [sb("res%d" % h, PACK * HALF, F32) for h in range(2)]
@@ -142,19 +140,26 @@ def tile_picked_csketch_silu_po_kernel(
         out_rows = out_0.rearrange("(p t) v -> p t v", t=PACK)
         out_words = out_1[0].rearrange("p c r -> p (c r)").bitcast(I32)
 
-        def look(n, h, t):
-            sign = signs[n, t // 2][:, (t % 2) * V + h * HALF : (t % 2) * V + (h + 1) * HALF]
-            offsets = hash_sb[n][:, h * HALF // 16 : (h + 1) * HALF // 16]
-            nc.vector.tensor_tensor(plane(looked[n, h], t, t + 1), y[t][:].indirect(offsets), sign, ALU.mult)
+        def look_pair(n, t):
+            cols = slice(t * V, (t + 1) * V)
+            nc.vector.tensor_tensor(pair[n][:, cols], y[t][:].indirect(hash_sb[n][:]), signs[n][:, cols], ALU.mult)
 
-        def low(h):
-            nc.vector.tensor_tensor(lo[h][:], looked[0, h][:], looked[1, h][:], ALU.min)
+        def look_third(h, t):
+            sign = signs[2][:, t * V + h * HALF : t * V + (h + 1) * HALF]
+            offsets = hash_sb[2][:, h * HALF // 16 : (h + 1) * HALF // 16]
+            nc.vector.tensor_tensor(plane(third[h], t, t + 1), y[t][:].indirect(offsets), sign, ALU.mult)
 
-        def high(h):
-            nc.vector.tensor_tensor(hi[h][:], looked[0, h][:], looked[1, h][:], ALU.max)
+        def keys(tile, h, t0, t1):
+            return tile[:].rearrange("p (t v) -> p t v", t=PACK)[:, t0:t1, h * HALF : (h + 1) * HALF]
+
+        def rows3(tile, t0, t1):
+            return tile[:].rearrange("p (t v) -> p t v", t=PACK)[:, t0:t1, :]
+
+        def bound(tiles, h, op):
+            nc.vector.tensor_tensor(rows3(tiles[h], 0, PACK), keys(pair[0], h, 0, PACK), keys(pair[1], h, 0, PACK), op)
 
         def cap(h, t0, t1):
-            nc.vector.tensor_tensor(plane(capped[h], t0, t1), plane(hi[h], t0, t1), plane(looked[2, h], t0, t1), ALU.min)
+            nc.vector.tensor_tensor(plane(capped[h], t0, t1), plane(hi[h], t0, t1), plane(third[h], t0, t1), ALU.min)
 
         def mid(h, t0, t1):
             nc.vector.tensor_tensor(plane(median[h], t0, t1), plane(lo[h], t0, t1), plane(capped[h], t0, t1), ALU.max)
@@ -186,8 +191,8 @@ def tile_picked_csketch_silu_po_kernel(
                 )
             return acc
 
-        def store_rows(h, t0, t1):
-            nc.sync.dma_start(
+        def store_rows(queue, h, t0, t1):
+            queue.dma_start(
                 out_rows[:, t0:t1, h * HALF : (h + 1) * HALF],
                 plane(res[h], t0, t1).rearrange("p (t v) -> p t v", v=HALF),
             )
@@ -197,53 +202,57 @@ def tile_picked_csketch_silu_po_kernel(
             nc.vector.quantize_mx(out=res_code[:, cols].bitcast(FP8X4), scales=res_scale[:, cols], in_=res_bf[h][:])
             nc.sync.dma_start(out_words[:, cols], res_code[:, cols].bitcast(I32))
 
-        for t in range(PACK):
-            for n in range(3):
-                look(n, 0, t)
-        low(0)
-        high(0)
-        look(0, 1, 0)
+        for n in range(2):
+            for t in range(PACK):
+                look_pair(n, t)
+        look_third(0, 0)
+        bound(hi, 0, ALU.max)
+        look_third(0, 1)
+        look_third(0, 2)
+        look_third(0, 3)
+        bound(lo, 0, ALU.min)
         cap(0, 0, PACK)
-        look(0, 1, 1)
+        bound(hi, 1, ALU.max)
         mid(0, 0, PACK)
         silu(0, 0, PACK)
-        look(0, 1, 2)
-        look(0, 1, 3)
+        bound(lo, 1, ALU.min)
+        w2_scale = keep.tile([P, N], U8, name="w2_scale", tag="sign1", align_bytes=64)
+        nc.vector.tensor_copy(
+            w2_scale[:].rearrange("p (t c i) -> p c t i", t=PACK, i=16),
+            w2_scale_raw[:].rearrange("p (c i t) -> p c t i", t=PACK, i=16),
+        )
+
         quantise_z(0)
-        looked[1, 1] = keep.tile([P, PACK * HALF], F32, name="looked1_1", tag="reused", align_bytes=64)
-        look(1, 1, 0)
+        third.append(keep.tile([P, PACK * HALF], F32, name="third1", tag="z_then_third", align_bytes=64))
+        look_third(1, 0)
+        look_third(1, 1)
         acc = second(0, 0, PACK)
         nc.scalar.copy(res[0][:], acc[:])
-        store_rows(0, 0, PACK)
+        store_rows(nc.sync, 0, 0, PACK)
+        cap(1, 0, 2)
+        look_third(1, 2)
+        mid(1, 0, 2)
+        silu(1, 0, 2)
         nc.scalar.copy(woven(res_bf[0], 0, PACK), planes(res[0][:], PACK))
-        look(1, 1, 1)
-        look(1, 1, 2)
-        look(1, 1, 3)
-        look(2, 1, 0)
-        low(1)
-        high(1)
-        look(2, 1, 1)
-        look(2, 1, 2)
-        cap(1, 0, 3)
-        look(2, 1, 3)
-        mid(1, 0, 3)
-        silu(1, 0, 3)
+        look_third(1, 3)
+        cap(1, 2, 3)
         cap(1, 3, 4)
-        quantise_res(0)
+        mid(1, 2, 3)
         mid(1, 3, 4)
-        silu(1, 3, 4)
+        silu(1, 2, 4)
         quantise_z(1)
+        quantise_res(0)
         acc_a = second(1, 0, 2)
         acc_b = second(1, 2, 4)
-        nc.scalar.copy(plane(res[1], 0, 2), acc_a[:])
-        store_rows(1, 0, 2)
+        nc.scalar.copy(woven(res_bf[1], 0, 2), planes(acc_a[:], 2))
         nc.vector.tensor_copy(woven(res_bf[1], 2, 4), planes(acc_b[:], 2))
-        nc.scalar.copy(plane(res[1], 2, 4), acc_b[:])
-        store_rows(1, 2, 4)
-        nc.vector.tensor_copy(woven(res_bf[1], 0, 2), planes(plane(res[1], 0, 2), 2))
         quantise_res(1)
+        nc.scalar.copy(plane(res[1], 0, 2), acc_a[:])
+        store_rows(nc.sync, 1, 0, 2)
+        nc.scalar.copy(plane(res[1], 2, 4), acc_b[:])
+        store_rows(nc.scalar, 1, 2, 4)
         for q in range(QUADS):
-            queue = nc.sync if q < 2 else nc.scalar
+            queue = nc.sync if q < 3 else nc.scalar
             queue.dma_start(
                 out_2[0, 4 * q : 4 * q + 4, :].bitcast(I32), res_scale[32 * q : 32 * q + 4, :].bitcast(I32)
             )

@@ -37,37 +37,36 @@ def tile_picked_csketch_silu_po_kernel(
         hash_sb = [lists.tile([P, V // 16], U16, name="hash%d" % n) for n in range(3)]
 
         x_scale_table = sb("x_scale_table", T, U8)
-        nc.gpsimd.memset(x_scale_table[:, : T // 2].bitcast(I32), 0)
-        nc.vector.memset(x_scale_table[:, T // 2 :].bitcast(I32), 0)
+        nc.vector.memset(x_scale_table[:].bitcast(I32), 0)
         warm_in = sb("warm_in", 8, F32)
         warm_out = sb("warm_out", 8, F32)
         nc.vector.memset(warm_in[:], 0.0)
         nc.scalar.activation(warm_out[:], warm_in[:], SILU)
 
-        nc.sync.dma_start(offs_sb[:], offs)
         w1_raw = keep.tile([P, PACK * H], F32, name="w1_raw", align_bytes=64)
         nc.sync.dma_start(w1_raw[:], w1.rearrange("(p j) c -> p (j c)", j=PACK))
+        nc.sync.dma_start(offs_sb[:], offs)
         for q in range(QUADS):
             nc.sync.dma_start(
-                x_scale_table[32 * q : 32 * q + 4, :].bitcast(I32), x_scales[0, 4 * q : 4 * q + 4, :].bitcast(I32)
+                x_scale_table[q:P:32, :].bitcast(I32), x_scales[0, q:16:4, :].bitcast(I32)
             )
         x_word_table = keep.tile([P, T], I32, name="x_word_table", tag="x_words_then_w1", align_bytes=64)
         nc.sync.dma_start(x_word_table[:], x_words[0].rearrange("p c r -> p (c r)").bitcast(I32))
         w2_word_raw = sb("w2_word_raw", N, I32)
         nc.sync.dma_start(w2_word_raw[:], w2_words[0].rearrange("p c r -> p (c r)").bitcast(I32))
 
-        for tile, h in zip(hash_sb, (h1, h2, h3)):
-            nc.sync.dma_start(tile[:], h)
         w2_scale_raw = sb("w2_scale_raw", N, U8)
-        nc.gpsimd.memset(w2_scale_raw[:].bitcast(I32), 0)
+        nc.vector.memset(w2_scale_raw[:].bitcast(I32), 0)
         signs = [
             keep.tile([P, PACK * V], F32, name="sign%d" % n, tag="sign%d" % n, align_bytes=64) for n in range(3)
         ]
+        for tile, h in zip(hash_sb, (h1, h2, h3)):
+            nc.sync.dma_start(tile[:], h)
         for tile, sg in zip(signs, (sg1, sg2, sg3)):
             nc.sync.dma_start(tile[:], sg.rearrange("(p t) v -> p (t v)", t=PACK))
         for q in range(QUADS):
             nc.sync.dma_start(
-                w2_scale_raw[32 * q : 32 * q + 4, :].bitcast(I32), w2_scales[0, 4 * q : 4 * q + 4, :].bitcast(I32)
+                w2_scale_raw[q:P:32, :].bitcast(I32), w2_scales[0, q:16:4, :].bitcast(I32)
             )
 
         w1_src = w1_raw[:].rearrange("p (j m t) -> p m t j", t=PACK, j=PACK)
@@ -75,42 +74,43 @@ def tile_picked_csketch_silu_po_kernel(
         w1_code = [sb("w1_code0", 2 * P, U32)]
         w1_scale = [sb("w1_scale%d" % a, 2 * P, U8) for a in range(2)]
         w1_dst = [tile[:].rearrange("p (t m j) -> p m t j", t=2, j=PACK) for tile in w1_bf]
-        nc.vector.tensor_copy(w1_dst[0], w1_src[:, :, 0:2, :])
+        nc.vector.tensor_copy(w1_dst[0][:, :80], w1_src[:, :80, 0:2, :])
+        nc.scalar.copy(w1_dst[0][:, 80:], w1_src[:, 80:, 0:2, :])
         nc.scalar.copy(w1_dst[1], w1_src[:, :, 2:4, :])
         x_scale = sb("x_scale", S, U8)
         nc.vector.tensor_copy(x_scale[:], x_scale_table[:].indirect(offs_sb[:]))
         nc.vector.quantize_mx(out=w1_code[0][:].bitcast(FP8X4), scales=w1_scale[0][:], in_=w1_bf[0][:])
 
-        x_word = [sb("x_word%d" % a, S // 2, U32) for a in range(2)]
+        x_word = sb("x_word", S, U32)
         for a in range(2):
             nc.vector.tensor_copy(
-                x_word[a][:], x_word_table[:].bitcast(U32).indirect(offs_sb[:, a * 16 : (a + 1) * 16])
+                x_word[:, a * 256 : (a + 1) * 256],
+                x_word_table[:].bitcast(U32).indirect(offs_sb[:, a * 16 : (a + 1) * 16]),
             )
 
         w1_code.append(keep.tile([P, 2 * P], U32, name="w1_code1", tag="x_words_then_w1", align_bytes=64))
         nc.vector.quantize_mx(out=w1_code[1][:].bitcast(FP8X4), scales=w1_scale[1][:], in_=w1_bf[1][:])
         y = [sb("y%d" % t, S, F32) for t in range(PACK)]
 
-        def first(acc, t, a):
+        def first(acc, t, cols):
             rows = slice(t % 2 * P, (t % 2 + 1) * P)
             nc.tensor.matmul_mx(
                 out=acc,
                 lhsT=w1_code[t // 2][:, rows].bitcast(FP8X4),
                 lhsT_scale=w1_scale[t // 2][:, rows],
-                rhs=x_word[a][:].bitcast(FP8X4),
-                rhs_scale=x_scale[:, a * 256 : (a + 1) * 256],
+                rhs=x_word[:, cols].bitcast(FP8X4),
+                rhs_scale=x_scale[:, cols],
                 start=True,
                 stop=True,
             )
 
         for a in range(2):
             acc = psum.tile([P, S // 2], F32, name="y_acc0_%d" % a)
-            first(acc[:], 0, a)
+            first(acc[:], 0, slice(a * 256, (a + 1) * 256))
             nc.scalar.copy(y[0][:, a * 256 : (a + 1) * 256], acc[:])
         for t in range(1, PACK):
             acc = psum.tile([P, S], F32, name="y_acc%d" % t)
-            for a in range(2):
-                first(acc[:, a * 256 : (a + 1) * 256], t, a)
+            first(acc[:], t, slice(0, S))
             nc.scalar.copy(y[t][:], acc[:])
 
         w2_word = sb("w2_word", N, I32)
@@ -126,11 +126,11 @@ def tile_picked_csketch_silu_po_kernel(
         hi = [sb("hi%d" % h, PACK * HALF, F32) for h in range(2)]
         third = [sb("third0", PACK * HALF, F32)]
         capped = [sb("capped%d" % h, PACK * HALF, F32) for h in range(2)]
-        median = [sb("median%d" % h, PACK * HALF, F32) for h in range(2)]
-        z_bf = [
-            keep.tile([P, PACK * HALF], BF16, name="z_bf0", tag="z_then_third", align_bytes=64),
-            sb("z_bf1", PACK * HALF, BF16),
+        median = [
+            keep.tile([P, PACK * HALF], F32, name="median0", tag="median_then_third", align_bytes=64),
+            sb("median1", PACK * HALF, F32),
         ]
+        z_bf = [sb("z_bf%d" % h, PACK * HALF, BF16) for h in range(2)]
         z_code = [sb("z_code%d" % h, HALF, U32) for h in range(2)]
         z_scale = [sb("z_scale%d" % h, HALF, U8) for h in range(2)]
         res = [sb("res%d" % h, PACK * HALF, F32) for h in range(2)]
@@ -223,7 +223,7 @@ def tile_picked_csketch_silu_po_kernel(
         )
 
         quantise_z(0)
-        third.append(keep.tile([P, PACK * HALF], F32, name="third1", tag="z_then_third", align_bytes=64))
+        third.append(keep.tile([P, PACK * HALF], F32, name="third1", tag="median_then_third", align_bytes=64))
         look_third(1, 0)
         look_third(1, 1)
         acc = second(0, 0, PACK)
@@ -254,5 +254,5 @@ def tile_picked_csketch_silu_po_kernel(
         for q in range(QUADS):
             queue = nc.sync if q < 3 else nc.scalar
             queue.dma_start(
-                out_2[0, 4 * q : 4 * q + 4, :].bitcast(I32), res_scale[32 * q : 32 * q + 4, :].bitcast(I32)
+                out_2[0, q:16:4, :].bitcast(I32), res_scale[q:P:32, :].bitcast(I32)
             )

@@ -19,6 +19,7 @@ P = 128
 PACK = 4
 QUADS = 4
 HALF = V // 2
+QUARTER = V // 4
 
 
 def tile_picked_csketch_silu_po_kernel(
@@ -36,61 +37,78 @@ def tile_picked_csketch_silu_po_kernel(
         offs_sb = lists.tile([P, S // 16], U16, name="offs_sb")
         hash_sb = [lists.tile([P, V // 16], U16, name="hash%d" % n) for n in range(3)]
 
-        x_scale_table = sb("x_scale_table", T, U8)
-        nc.vector.memset(x_scale_table[:].bitcast(I32), 0)
+        def words(ap):
+            return ap.bitcast(I32)
+
+        def shared(name, cols, dtype, tag):
+            return keep.tile([P, cols], dtype, name=name, tag=tag, align_bytes=64)
+
+        def place_scale_rows(plane_tile, spread_tile):
+            for r in range(QUADS):
+                nc.sync.dma_start(words(plane_tile[r:P:32, :]), words(spread_tile[8 * r : P : 32, :]))
+
+        x_scale_table = shared("x_scale_table", T, U8, "x_scale_table")
+        w2_scale_raw = sb("w2_scale_raw", N, U8)
+        x_scale = sb("x_scale", S, U8)
+        for tile in (x_scale_table, w2_scale_raw, x_scale):
+            nc.vector.memset(words(tile[:]), 0)
         warm_in = sb("warm_in", 8, F32)
         warm_out = sb("warm_out", 8, F32)
         nc.vector.memset(warm_in[:], 0.0)
         nc.scalar.activation(warm_out[:], warm_in[:], SILU)
 
-        w1_raw = keep.tile([P, PACK * H], F32, name="w1_raw", align_bytes=64)
-        nc.sync.dma_start(w1_raw[:], w1.rearrange("(p j) c -> p (j c)", j=PACK))
+        w1_rows = w1.rearrange("(p j) c -> p (j c)", j=PACK)
+        w1_raw = [shared("w1_raw%d" % b, 2 * H, F32, "w1_raw%d" % b) for b in range(2)]
+        nc.sync.dma_start(w1_raw[0][:], w1_rows[:, : 2 * H])
         nc.sync.dma_start(offs_sb[:], offs)
-        for q in range(QUADS):
-            nc.sync.dma_start(
-                x_scale_table[q:P:32, :].bitcast(I32), x_scales[0, q:16:4, :].bitcast(I32)
-            )
-        x_word_table = keep.tile([P, T], I32, name="x_word_table", tag="x_words_then_w1", align_bytes=64)
-        nc.sync.dma_start(x_word_table[:], x_words[0].rearrange("p c r -> p (c r)").bitcast(I32))
-        w2_word_raw = sb("w2_word_raw", N, I32)
-        nc.sync.dma_start(w2_word_raw[:], w2_words[0].rearrange("p c r -> p (c r)").bitcast(I32))
-
-        w2_scale_raw = sb("w2_scale_raw", N, U8)
-        nc.vector.memset(w2_scale_raw[:].bitcast(I32), 0)
-        signs = [
-            keep.tile([P, PACK * V], F32, name="sign%d" % n, tag="sign%d" % n, align_bytes=64) for n in range(3)
-        ]
+        nc.sync.dma_start(words(x_scale_table[0:P:8, :]), words(x_scales[0]))
+        nc.sync.dma_start(words(w2_scale_raw[0:P:8, :]), words(w2_scales[0]))
         for tile, h in zip(hash_sb, (h1, h2, h3)):
             nc.sync.dma_start(tile[:], h)
-        for tile, sg in zip(signs, (sg1, sg2, sg3)):
-            nc.sync.dma_start(tile[:], sg.rearrange("(p t) v -> p (t v)", t=PACK))
-        for q in range(QUADS):
-            nc.sync.dma_start(
-                w2_scale_raw[q:P:32, :].bitcast(I32), w2_scales[0, q:16:4, :].bitcast(I32)
-            )
+        x_word_table = shared("x_word_table", T, I32, "x_word_table")
+        nc.sync.dma_start(x_word_table[:], words(x_words[0].rearrange("p c r -> p (c r)")))
+        nc.sync.dma_start(w1_raw[1][:], w1_rows[:, 2 * H :])
 
-        w1_src = w1_raw[:].rearrange("p (j m t) -> p m t j", t=PACK, j=PACK)
-        w1_bf = [sb("w1_bf%d" % a, 2 * H, BF16) for a in range(2)]
-        w1_code = [sb("w1_code0", 2 * P, U32)]
+        x_scale_spread = sb("x_scale_spread", S, U8)
+        nc.vector.tensor_copy(x_scale_spread[:], x_scale_table[:].indirect(offs_sb[:]))
+        place_scale_rows(x_scale, x_scale_spread)
+        w2_word_raw = shared("w2_word_raw", N, I32, "x_scale_table")
+        nc.sync.dma_start(w2_word_raw[:], words(w2_words[0].rearrange("p c r -> p (c r)")))
+        w2_scale_spread = sb("w2_scale_spread", N, U8)
+        nc.vector.tensor_copy(
+            w2_scale_spread[:].rearrange("p (t c i) -> p c t i", t=PACK, i=16),
+            w2_scale_raw[:].rearrange("p (c i t) -> p c t i", t=PACK, i=16),
+        )
+
+        w1_src = [tile[:].rearrange("p (j m t) -> p m t j", t=PACK, j=2) for tile in w1_raw]
+        w1_bf = [shared("w1_bf%d" % a, 2 * H, BF16, "w1_bf%d" % a) for a in range(2)]
+        w1_code = [sb("w1_code%d" % a, 2 * P, U32) for a in range(2)]
         w1_scale = [sb("w1_scale%d" % a, 2 * P, U8) for a in range(2)]
         w1_dst = [tile[:].rearrange("p (t m j) -> p m t j", t=2, j=PACK) for tile in w1_bf]
-        nc.vector.tensor_copy(w1_dst[0][:, :80], w1_src[:, :80, 0:2, :])
-        nc.scalar.copy(w1_dst[0][:, 80:], w1_src[:, 80:, 0:2, :])
-        nc.scalar.copy(w1_dst[1], w1_src[:, :, 2:4, :])
-        x_scale = sb("x_scale", S, U8)
-        nc.vector.tensor_copy(x_scale[:], x_scale_table[:].indirect(offs_sb[:]))
-        nc.vector.quantize_mx(out=w1_code[0][:].bitcast(FP8X4), scales=w1_scale[0][:], in_=w1_bf[0][:])
-
+        nc.scalar.copy(w1_dst[0][:, :, :, 0:2], w1_src[0][:, :, 0:2, :])
+        nc.scalar.copy(w1_dst[1][:, :, :, 0:2], w1_src[0][:, :, 2:4, :])
+        sign_rows = [sg.rearrange("(p t) v -> p (t v)", t=PACK) for sg in (sg1, sg2, sg3)]
+        signs = [shared("sign0", PACK * V, F32, "w1_raw0")]
+        nc.sync.dma_start(signs[0][:, : 2 * V], sign_rows[0][:, : 2 * V])
+        nc.sync.dma_start(signs[0][:, 2 * V :], sign_rows[0][:, 2 * V :])
         x_word = sb("x_word", S, U32)
-        for a in range(2):
-            nc.vector.tensor_copy(
-                x_word[:, a * 256 : (a + 1) * 256],
-                x_word_table[:].bitcast(U32).indirect(offs_sb[:, a * 16 : (a + 1) * 16]),
-            )
+        nc.vector.tensor_copy(x_word[:], x_word_table[:].bitcast(U32).indirect(offs_sb[:]))
+        signs.append(shared("sign1", PACK * V, F32, "x_word_table"))
+        nc.sync.dma_start(signs[1][:], sign_rows[1])
 
-        w1_code.append(keep.tile([P, 2 * P], U32, name="w1_code1", tag="x_words_then_w1", align_bytes=64))
+        nc.vector.tensor_copy(w1_dst[0][:, :96, :, 2:4], w1_src[1][:, :96, 0:2, :])
+        nc.scalar.copy(w1_dst[0][:, 96:, :, 2:4], w1_src[1][:, 96:, 0:2, :])
+        nc.scalar.copy(w1_dst[1][:, :, :, 2:4], w1_src[1][:, :, 2:4, :])
+        signs.append(shared("sign2", PACK * V, F32, "w1_raw1"))
+        nc.sync.dma_start(signs[2][:], sign_rows[2])
+        for t in range(2):
+            nc.vector.quantize_mx(
+                out=w1_code[0][:, t * P : (t + 1) * P].bitcast(FP8X4),
+                scales=w1_scale[0][:, t * P : (t + 1) * P],
+                in_=w1_bf[0][:, t * H : (t + 1) * H],
+            )
         nc.vector.quantize_mx(out=w1_code[1][:].bitcast(FP8X4), scales=w1_scale[1][:], in_=w1_bf[1][:])
-        y = [sb("y%d" % t, S, F32) for t in range(PACK)]
+        y = [keep.tile([P, S], F32, name="y%d" % t, tag="y%d" % t, align_bytes=64) for t in range(PACK)]
 
         def first(acc, t, cols):
             rows = slice(t % 2 * P, (t % 2 + 1) * P)
@@ -113,23 +131,17 @@ def tile_picked_csketch_silu_po_kernel(
             first(acc[:], t, slice(0, S))
             nc.scalar.copy(y[t][:], acc[:])
 
+        w2_scale = shared("w2_scale", N, U8, "w1_bf1")
+        nc.gpsimd.memset(words(w2_scale[:]), 0)
+        place_scale_rows(w2_scale, w2_scale_spread)
         w2_word = sb("w2_word", N, I32)
         nc.vector.tensor_copy(
             w2_word[:].rearrange("p (t c i) -> p c t i", t=PACK, i=4),
             w2_word_raw[:].rearrange("p (c i t) -> p c t i", t=PACK, i=4),
         )
-        def plane(tile, t0, t1):
-            return tile[:, t0 * HALF : t1 * HALF]
-
-        pair = [sb("pair%d" % n, PACK * V, F32) for n in range(2)]
-        lo = [sb("lo%d" % h, PACK * HALF, F32) for h in range(2)]
-        hi = [sb("hi%d" % h, PACK * HALF, F32) for h in range(2)]
-        third = [sb("third0", PACK * HALF, F32)]
+        looked = [sb("looked%d" % n, PACK * V, F32) for n in range(3)]
         capped = [sb("capped%d" % h, PACK * HALF, F32) for h in range(2)]
-        median = [
-            keep.tile([P, PACK * HALF], F32, name="median0", tag="median_then_third", align_bytes=64),
-            sb("median1", PACK * HALF, F32),
-        ]
+        median = [sb("median%d" % h, PACK * HALF, F32) for h in range(2)]
         z_bf = [sb("z_bf%d" % h, PACK * HALF, BF16) for h in range(2)]
         z_code = [sb("z_code%d" % h, HALF, U32) for h in range(2)]
         z_scale = [sb("z_scale%d" % h, HALF, U8) for h in range(2)]
@@ -140,38 +152,38 @@ def tile_picked_csketch_silu_po_kernel(
         out_rows = out_0.rearrange("(p t) v -> p t v", t=PACK)
         out_words = out_1[0].rearrange("p c r -> p (c r)").bitcast(I32)
 
-        def look_pair(n, t):
+        def plane(tile, t0, t1):
+            return tile[:, t0 * HALF : t1 * HALF]
+
+        def look(n, t):
             cols = slice(t * V, (t + 1) * V)
-            nc.vector.tensor_tensor(pair[n][:, cols], y[t][:].indirect(hash_sb[n][:]), signs[n][:, cols], ALU.mult)
+            nc.vector.tensor_tensor(looked[n][:, cols], y[t][:].indirect(hash_sb[n][:]), signs[n][:, cols], ALU.mult)
 
-        def look_third(h, t):
-            sign = signs[2][:, t * V + h * HALF : t * V + (h + 1) * HALF]
-            offsets = hash_sb[2][:, h * HALF // 16 : (h + 1) * HALF // 16]
-            nc.vector.tensor_tensor(plane(third[h], t, t + 1), y[t][:].indirect(offsets), sign, ALU.mult)
+        def keys(tile, k0, k1):
+            return tile[:].rearrange("p (t v) -> p t v", t=PACK)[:, :, k0:k1]
 
-        def keys(tile, h, t0, t1):
-            return tile[:].rearrange("p (t v) -> p t v", t=PACK)[:, t0:t1, h * HALF : (h + 1) * HALF]
+        def bound(name, tag, h, op):
+            tile = keep.tile([P, PACK * HALF], F32, name=name, tag=tag, align_bytes=64)
+            k0, k1 = h * HALF, (h + 1) * HALF
+            nc.vector.tensor_tensor(keys(tile, 0, HALF), keys(looked[0], k0, k1), keys(looked[1], k0, k1), op)
+            return tile
 
-        def rows3(tile, t0, t1):
-            return tile[:].rearrange("p (t v) -> p t v", t=PACK)[:, t0:t1, :]
+        def cap(h, hi, k0, k1):
+            third = keys(looked[2], h * HALF + k0, h * HALF + k1)
+            nc.vector.tensor_tensor(keys(capped[h], k0, k1), keys(hi, k0, k1), third, ALU.min)
 
-        def bound(tiles, h, op):
-            nc.vector.tensor_tensor(rows3(tiles[h], 0, PACK), keys(pair[0], h, 0, PACK), keys(pair[1], h, 0, PACK), op)
+        def mid(h, lo, k0, k1):
+            nc.vector.tensor_tensor(keys(median[h], k0, k1), keys(lo, k0, k1), keys(capped[h], k0, k1), ALU.max)
 
-        def cap(h, t0, t1):
-            nc.vector.tensor_tensor(plane(capped[h], t0, t1), plane(hi[h], t0, t1), plane(third[h], t0, t1), ALU.min)
-
-        def mid(h, t0, t1):
-            nc.vector.tensor_tensor(plane(median[h], t0, t1), plane(lo[h], t0, t1), plane(capped[h], t0, t1), ALU.max)
-
-        def woven(tile, t0, t1):
-            return tile[:].rearrange("p (c i t) -> p c t i", t=PACK, i=4)[:, :, t0:t1, :]
+        def woven(tile):
+            return tile[:].rearrange("p (c i t) -> p c t i", t=PACK, i=4)
 
         def planes(ap, count):
             return ap.rearrange("p (t c i) -> p c t i", t=count, i=4)
 
-        def silu(h, t0, t1):
-            nc.scalar.activation(woven(z_bf[h], t0, t1), planes(plane(median[h], t0, t1), t1 - t0), SILU)
+        def silu(h, k0, k1):
+            groups = slice(k0 // 4, k1 // 4)
+            nc.scalar.activation(woven(z_bf[h])[:, groups], planes(median[h][:], PACK)[:, groups], SILU)
 
         def quantise_z(h):
             nc.vector.quantize_mx(out=z_code[h][:].bitcast(FP8X4), scales=z_scale[h][:], in_=z_bf[h][:])
@@ -200,59 +212,44 @@ def tile_picked_csketch_silu_po_kernel(
         def quantise_res(h):
             cols = slice(h * HALF, (h + 1) * HALF)
             nc.vector.quantize_mx(out=res_code[:, cols].bitcast(FP8X4), scales=res_scale[:, cols], in_=res_bf[h][:])
-            nc.sync.dma_start(out_words[:, cols], res_code[:, cols].bitcast(I32))
 
         for n in range(2):
             for t in range(PACK):
-                look_pair(n, t)
-        look_third(0, 0)
-        bound(hi, 0, ALU.max)
-        look_third(0, 1)
-        look_third(0, 2)
-        look_third(0, 3)
-        bound(lo, 0, ALU.min)
-        cap(0, 0, PACK)
-        bound(hi, 1, ALU.max)
-        mid(0, 0, PACK)
-        silu(0, 0, PACK)
-        bound(lo, 1, ALU.min)
-        w2_scale = keep.tile([P, N], U8, name="w2_scale", tag="sign1", align_bytes=64)
-        nc.vector.tensor_copy(
-            w2_scale[:].rearrange("p (t c i) -> p c t i", t=PACK, i=16),
-            w2_scale_raw[:].rearrange("p (c i t) -> p c t i", t=PACK, i=16),
-        )
-
+                look(n, t)
+        hi0 = bound("hi0", "hi0", 0, ALU.max)
+        for t in range(PACK):
+            look(2, t)
+        lo0 = bound("lo0", "y2", 0, ALU.min)
+        cap(0, hi0, 0, HALF)
+        hi1 = bound("hi1", "y3", 1, ALU.max)
+        mid(0, lo0, 0, HALF)
+        silu(0, 0, HALF)
+        lo1 = bound("lo1", "hi0", 1, ALU.min)
+        cap(1, hi1, 0, QUARTER)
         quantise_z(0)
-        third.append(keep.tile([P, PACK * HALF], F32, name="third1", tag="median_then_third", align_bytes=64))
-        look_third(1, 0)
-        look_third(1, 1)
         acc = second(0, 0, PACK)
+        cap(1, hi1, QUARTER, HALF)
+        mid(1, lo1, 0, QUARTER)
+        silu(1, 0, QUARTER)
+        mid(1, lo1, QUARTER, HALF)
+        silu(1, QUARTER, HALF)
+        nc.vector.tensor_copy(woven(res_bf[0]), planes(acc[:], PACK))
+        quantise_z(1)
         nc.scalar.copy(res[0][:], acc[:])
         store_rows(nc.sync, 0, 0, PACK)
-        cap(1, 0, 2)
-        look_third(1, 2)
-        mid(1, 0, 2)
-        silu(1, 0, 2)
-        nc.scalar.copy(woven(res_bf[0], 0, PACK), planes(res[0][:], PACK))
-        look_third(1, 3)
-        cap(1, 2, 3)
-        cap(1, 3, 4)
-        mid(1, 2, 3)
-        mid(1, 3, 4)
-        silu(1, 2, 4)
-        quantise_z(1)
         quantise_res(0)
         acc_a = second(1, 0, 2)
         acc_b = second(1, 2, 4)
-        nc.scalar.copy(woven(res_bf[1], 0, 2), planes(acc_a[:], 2))
-        nc.vector.tensor_copy(woven(res_bf[1], 2, 4), planes(acc_b[:], 2))
-        quantise_res(1)
-        nc.scalar.copy(plane(res[1], 0, 2), acc_a[:])
+        nc.vector.tensor_copy(woven(res_bf[1])[:, :, 0:2], planes(acc_a[:], 2))
+        nc.scalar.copy(woven(res_bf[1])[:, :, 2:4], planes(acc_b[:], 2))
+        nc.vector.tensor_copy(plane(res[1], 0, 2), acc_a[:])
         store_rows(nc.sync, 1, 0, 2)
         nc.scalar.copy(plane(res[1], 2, 4), acc_b[:])
         store_rows(nc.scalar, 1, 2, 4)
+        quantise_res(1)
+        nc.sync.dma_start(out_words, res_code[:].bitcast(I32))
         for q in range(QUADS):
-            queue = nc.sync if q < 3 else nc.scalar
+            queue = nc.sync if q < 2 else nc.scalar
             queue.dma_start(
                 out_2[0, q:16:4, :].bitcast(I32), res_scale[q:P:32, :].bitcast(I32)
             )

@@ -82,7 +82,7 @@ def tile_picked_csketch_silu_po_kernel(
 
         w1_src = [tile[:].rearrange("p (j m t) -> p m t j", t=PACK, j=2) for tile in w1_raw]
         w1_bf = [shared("w1_bf%d" % a, 2 * H, BF16, "w1_bf%d" % a) for a in range(2)]
-        w1_code = [sb("w1_code%d" % a, 2 * P, U32) for a in range(2)]
+        w1_code = [sb("w1_code0", 2 * P, U32)]
         w1_scale = [sb("w1_scale%d" % a, 2 * P, U8) for a in range(2)]
         w1_dst = [tile[:].rearrange("p (t m j) -> p m t j", t=2, j=PACK) for tile in w1_bf]
         nc.scalar.copy(w1_dst[0][:, :, :, 0:2], w1_src[0][:, :, 0:2, :])
@@ -94,7 +94,8 @@ def tile_picked_csketch_silu_po_kernel(
         x_word = sb("x_word", S, U32)
         nc.vector.tensor_copy(x_word[:], x_word_table[:].bitcast(U32).indirect(offs_sb[:]))
         signs.append(shared("sign1", PACK * V, F32, "x_word_table"))
-        nc.sync.dma_start(signs[1][:], sign_rows[1])
+        nc.sync.dma_start(signs[1][:, : 2 * V], sign_rows[1][:, : 2 * V])
+        nc.sync.dma_start(signs[1][:, 2 * V :], sign_rows[1][:, 2 * V :])
 
         nc.vector.tensor_copy(w1_dst[0][:, :96, :, 2:4], w1_src[1][:, :96, 0:2, :])
         nc.scalar.copy(w1_dst[0][:, 96:, :, 2:4], w1_src[1][:, 96:, 0:2, :])
@@ -107,7 +108,16 @@ def tile_picked_csketch_silu_po_kernel(
                 scales=w1_scale[0][:, t * P : (t + 1) * P],
                 in_=w1_bf[0][:, t * H : (t + 1) * H],
             )
+        w2_word = sb("w2_word", N, I32)
+        nc.vector.tensor_copy(
+            w2_word[:].rearrange("p (t c i) -> p c t i", t=PACK, i=4),
+            w2_word_raw[:].rearrange("p (c i t) -> p c t i", t=PACK, i=4),
+        )
+        w1_code.append(shared("w1_code1", 2 * P, U32, "x_scale_table"))
         nc.vector.quantize_mx(out=w1_code[1][:].bitcast(FP8X4), scales=w1_scale[1][:], in_=w1_bf[1][:])
+        w2_scale = shared("w2_scale", N, U8, "w1_bf0")
+        nc.vector.memset(words(w2_scale[:]), 0)
+        place_scale_rows(w2_scale, w2_scale_spread)
         y = [keep.tile([P, S], F32, name="y%d" % t, tag="y%d" % t, align_bytes=64) for t in range(PACK)]
 
         def first(acc, t, cols):
@@ -131,15 +141,7 @@ def tile_picked_csketch_silu_po_kernel(
             first(acc[:], t, slice(0, S))
             nc.scalar.copy(y[t][:], acc[:])
 
-        w2_scale = shared("w2_scale", N, U8, "w1_bf1")
-        nc.gpsimd.memset(words(w2_scale[:]), 0)
-        place_scale_rows(w2_scale, w2_scale_spread)
-        w2_word = sb("w2_word", N, I32)
-        nc.vector.tensor_copy(
-            w2_word[:].rearrange("p (t c i) -> p c t i", t=PACK, i=4),
-            w2_word_raw[:].rearrange("p (c i t) -> p c t i", t=PACK, i=4),
-        )
-        looked = [sb("looked%d" % n, PACK * V, F32) for n in range(3)]
+        looked = [shared("looked0", PACK * V, F32, "w1_bf1")] + [sb("looked%d" % n, PACK * V, F32) for n in (1, 2)]
         capped = [sb("capped%d" % h, PACK * HALF, F32) for h in range(2)]
         median = [sb("median%d" % h, PACK * HALF, F32) for h in range(2)]
         z_bf = [sb("z_bf%d" % h, PACK * HALF, BF16) for h in range(2)]
@@ -213,18 +215,20 @@ def tile_picked_csketch_silu_po_kernel(
             cols = slice(h * HALF, (h + 1) * HALF)
             nc.vector.quantize_mx(out=res_code[:, cols].bitcast(FP8X4), scales=res_scale[:, cols], in_=res_bf[h][:])
 
-        for n in range(2):
-            for t in range(PACK):
-                look(n, t)
-        hi0 = bound("hi0", "hi0", 0, ALU.max)
         for t in range(PACK):
-            look(2, t)
+            for n in range(2):
+                look(n, t)
+        look(2, 0)
+        look(2, 1)
+        hi0 = bound("hi0", "y0", 0, ALU.max)
+        look(2, 2)
+        look(2, 3)
         lo0 = bound("lo0", "y2", 0, ALU.min)
         cap(0, hi0, 0, HALF)
         hi1 = bound("hi1", "y3", 1, ALU.max)
         mid(0, lo0, 0, HALF)
         silu(0, 0, HALF)
-        lo1 = bound("lo1", "hi0", 1, ALU.min)
+        lo1 = bound("lo1", "y0", 1, ALU.min)
         cap(1, hi1, 0, QUARTER)
         quantise_z(0)
         acc = second(0, 0, PACK)

@@ -63,11 +63,12 @@ def tile_picked_csketch_silu_po_kernel(
         nc.sync.dma_start(offs_sb[:], offs)
         nc.sync.dma_start(words(x_scale_table[0:P:8, :]), words(x_scales[0]))
         nc.sync.dma_start(words(w2_scale_raw[0:P:8, :]), words(w2_scales[0]))
-        for tile, h in zip(hash_sb, (h1, h2, h3)):
-            nc.sync.dma_start(tile[:], h)
+        nc.sync.dma_start(hash_sb[0][:], h1)
         x_word_table = shared("x_word_table", T, I32, "x_word_table")
         nc.sync.dma_start(x_word_table[:], words(x_words[0].rearrange("p c r -> p (c r)")))
         nc.sync.dma_start(w1_raw[1][:], w1_rows[:, 2 * H :])
+        for tile, h in zip(hash_sb[1:], (h2, h3)):
+            nc.sync.dma_start(tile[:], h)
 
         x_scale_spread = sb("x_scale_spread", S, U8)
         nc.vector.tensor_copy(x_scale_spread[:], x_scale_table[:].indirect(offs_sb[:]))
@@ -88,20 +89,20 @@ def tile_picked_csketch_silu_po_kernel(
         nc.scalar.copy(w1_dst[0][:, :, :, 0:2], w1_src[0][:, :, 0:2, :])
         nc.scalar.copy(w1_dst[1][:, :, :, 0:2], w1_src[0][:, :, 2:4, :])
         sign_rows = [sg.rearrange("(p t) v -> p (t v)", t=PACK) for sg in (sg1, sg2, sg3)]
-        signs = [shared("sign0", PACK * V, F32, "w1_raw0")]
-        nc.sync.dma_start(signs[0][:, : 2 * V], sign_rows[0][:, : 2 * V])
-        nc.sync.dma_start(signs[0][:, 2 * V :], sign_rows[0][:, 2 * V :])
+        early_signs = shared("early_signs", PACK * V, F32, "w1_raw0")
+        for n in range(2):
+            nc.sync.dma_start(early_signs[:, n * 2 * V : (n + 1) * 2 * V], sign_rows[n][:, : 2 * V])
         x_word = sb("x_word", S, U32)
         nc.vector.tensor_copy(x_word[:], x_word_table[:].bitcast(U32).indirect(offs_sb[:]))
-        signs.append(shared("sign1", PACK * V, F32, "x_word_table"))
-        nc.sync.dma_start(signs[1][:, : 2 * V], sign_rows[1][:, : 2 * V])
-        nc.sync.dma_start(signs[1][:, 2 * V :], sign_rows[1][:, 2 * V :])
+        late_signs = shared("late_signs", PACK * V, F32, "x_word_table")
+        for n in range(2):
+            nc.sync.dma_start(late_signs[:, n * 2 * V : (n + 1) * 2 * V], sign_rows[n][:, 2 * V :])
 
         nc.vector.tensor_copy(w1_dst[0][:, :96, :, 2:4], w1_src[1][:, :96, 0:2, :])
         nc.scalar.copy(w1_dst[0][:, 96:, :, 2:4], w1_src[1][:, 96:, 0:2, :])
         nc.scalar.copy(w1_dst[1][:, :, :, 2:4], w1_src[1][:, :, 2:4, :])
-        signs.append(shared("sign2", PACK * V, F32, "w1_raw1"))
-        nc.sync.dma_start(signs[2][:], sign_rows[2])
+        third_signs = shared("third_signs", PACK * V, F32, "w1_raw1")
+        nc.sync.dma_start(third_signs[:], sign_rows[2])
         for t in range(2):
             nc.vector.quantize_mx(
                 out=w1_code[0][:, t * P : (t + 1) * P].bitcast(FP8X4),
@@ -159,7 +160,12 @@ def tile_picked_csketch_silu_po_kernel(
 
         def look(n, t):
             cols = slice(t * V, (t + 1) * V)
-            nc.vector.tensor_tensor(looked[n][:, cols], y[t][:].indirect(hash_sb[n][:]), signs[n][:, cols], ALU.mult)
+            if n == 2:
+                sign = third_signs[:, cols]
+            else:
+                start = (2 * n + t % 2) * V
+                sign = (early_signs if t < 2 else late_signs)[:, start : start + V]
+            nc.vector.tensor_tensor(looked[n][:, cols], y[t][:].indirect(hash_sb[n][:]), sign, ALU.mult)
 
         def keys(tile, k0, k1):
             return tile[:].rearrange("p (t v) -> p t v", t=PACK)[:, :, k0:k1]

@@ -63,9 +63,9 @@ def tile_picked_csketch_silu_po_kernel(
         nc.sync.dma_start(offs_sb[:], offs)
         nc.sync.dma_start(words(x_scale_table[0:P:8, :]), words(x_scales[0]))
         nc.sync.dma_start(words(w2_scale_raw[0:P:8, :]), words(w2_scales[0]))
-        nc.sync.dma_start(hash_sb[0][:], h1)
         x_word_table = shared("x_word_table", T, I32, "x_word_table")
         nc.sync.dma_start(x_word_table[:], words(x_words[0].rearrange("p c r -> p (c r)")))
+        nc.sync.dma_start(hash_sb[0][:], h1)
         nc.sync.dma_start(w1_raw[1][:], w1_rows[:, 2 * H :])
         for tile, h in zip(hash_sb[1:], (h2, h3)):
             nc.sync.dma_start(tile[:], h)
@@ -109,13 +109,13 @@ def tile_picked_csketch_silu_po_kernel(
                 scales=w1_scale[0][:, t * P : (t + 1) * P],
                 in_=w1_bf[0][:, t * H : (t + 1) * H],
             )
+        w1_code.append(sb("w1_code1", 2 * P, U32))
+        nc.vector.quantize_mx(out=w1_code[1][:].bitcast(FP8X4), scales=w1_scale[1][:], in_=w1_bf[1][:])
         w2_word = sb("w2_word", N, I32)
         nc.vector.tensor_copy(
             w2_word[:].rearrange("p (t c i) -> p c t i", t=PACK, i=4),
             w2_word_raw[:].rearrange("p (c i t) -> p c t i", t=PACK, i=4),
         )
-        w1_code.append(shared("w1_code1", 2 * P, U32, "x_scale_table"))
-        nc.vector.quantize_mx(out=w1_code[1][:].bitcast(FP8X4), scales=w1_scale[1][:], in_=w1_bf[1][:])
         w2_scale = shared("w2_scale", N, U8, "w1_bf0")
         nc.vector.memset(words(w2_scale[:]), 0)
         place_scale_rows(w2_scale, w2_scale_spread)
@@ -134,7 +134,7 @@ def tile_picked_csketch_silu_po_kernel(
             )
 
         for a in range(2):
-            acc = psum.tile([P, S // 2], F32, name="y_acc0_%d" % a)
+            acc = psum.tile([P, S // 2], F32, name="y_acc0_%d" % a, tag="y_acc0_%d" % a)
             first(acc[:], 0, slice(a * 256, (a + 1) * 256))
             nc.scalar.copy(y[0][:, a * 256 : (a + 1) * 256], acc[:])
         for t in range(1, PACK):
@@ -142,7 +142,7 @@ def tile_picked_csketch_silu_po_kernel(
             first(acc[:], t, slice(0, S))
             nc.scalar.copy(y[t][:], acc[:])
 
-        looked = [shared("looked0", PACK * V, F32, "w1_bf1")] + [sb("looked%d" % n, PACK * V, F32) for n in (1, 2)]
+        looked = [shared("looked0", PACK * V, F32, "x_scale_table")] + [sb("looked%d" % n, PACK * V, F32) for n in (1, 2)]
         capped = [sb("capped%d" % h, PACK * HALF, F32) for h in range(2)]
         median = [sb("median%d" % h, PACK * HALF, F32) for h in range(2)]
         z_bf = [sb("z_bf%d" % h, PACK * HALF, BF16) for h in range(2)]
@@ -170,18 +170,18 @@ def tile_picked_csketch_silu_po_kernel(
         def keys(tile, k0, k1):
             return tile[:].rearrange("p (t v) -> p t v", t=PACK)[:, :, k0:k1]
 
-        def bound(name, tag, h, op):
-            tile = keep.tile([P, PACK * HALF], F32, name=name, tag=tag, align_bytes=64)
-            k0, k1 = h * HALF, (h + 1) * HALF
-            nc.vector.tensor_tensor(keys(tile, 0, HALF), keys(looked[0], k0, k1), keys(looked[1], k0, k1), op)
+        def bound(name, tag, op):
+            tile = keep.tile([P, PACK * V], F32, name=name, tag=tag, align_bytes=64)
+            nc.vector.tensor_tensor(tile[:], looked[0][:], looked[1][:], op)
             return tile
 
         def cap(h, hi, k0, k1):
-            third = keys(looked[2], h * HALF + k0, h * HALF + k1)
-            nc.vector.tensor_tensor(keys(capped[h], k0, k1), keys(hi, k0, k1), third, ALU.min)
+            high, third = [keys(tile, h * HALF + k0, h * HALF + k1) for tile in (hi, looked[2])]
+            nc.vector.tensor_tensor(keys(capped[h], k0, k1), high, third, ALU.min)
 
         def mid(h, lo, k0, k1):
-            nc.vector.tensor_tensor(keys(median[h], k0, k1), keys(lo, k0, k1), keys(capped[h], k0, k1), ALU.max)
+            low = keys(lo, h * HALF + k0, h * HALF + k1)
+            nc.vector.tensor_tensor(keys(median[h], k0, k1), low, keys(capped[h], k0, k1), ALU.max)
 
         def woven(tile):
             return tile[:].rearrange("p (c i t) -> p c t i", t=PACK, i=4)
@@ -196,8 +196,8 @@ def tile_picked_csketch_silu_po_kernel(
         def quantise_z(h):
             nc.vector.quantize_mx(out=z_code[h][:].bitcast(FP8X4), scales=z_scale[h][:], in_=z_bf[h][:])
 
-        def second(h, t0, t1):
-            acc = psum.tile([P, (t1 - t0) * HALF], F32, name="out_acc%d_%d" % (h, t0))
+        def second(h, t0, t1, tag):
+            acc = psum.tile([P, (t1 - t0) * HALF], F32, name="out_acc%d_%d" % (h, t0), tag=tag)
             for t in range(t0, t1):
                 rows = slice(t * P, (t + 1) * P)
                 nc.tensor.matmul_mx(
@@ -226,36 +226,36 @@ def tile_picked_csketch_silu_po_kernel(
                 look(n, t)
         look(2, 0)
         look(2, 1)
-        hi0 = bound("hi0", "y0", 0, ALU.max)
+        hi = bound("hi", "y0", ALU.max)
         look(2, 2)
         look(2, 3)
-        lo0 = bound("lo0", "y2", 0, ALU.min)
-        cap(0, hi0, 0, HALF)
-        hi1 = bound("hi1", "y3", 1, ALU.max)
-        mid(0, lo0, 0, HALF)
+        lo = bound("lo", "y2", ALU.min)
+        cap(0, hi, 0, HALF)
+        cap(1, hi, 0, QUARTER)
+        mid(0, lo, 0, HALF)
         silu(0, 0, HALF)
-        lo1 = bound("lo1", "y0", 1, ALU.min)
-        cap(1, hi1, 0, QUARTER)
+        cap(1, hi, QUARTER, HALF)
+        for k0 in (0, QUARTER):
+            mid(1, lo, k0, k0 + QUARTER)
+            silu(1, k0, k0 + QUARTER)
         quantise_z(0)
-        acc = second(0, 0, PACK)
-        cap(1, hi1, QUARTER, HALF)
-        mid(1, lo1, 0, QUARTER)
-        silu(1, 0, QUARTER)
-        mid(1, lo1, QUARTER, HALF)
-        silu(1, QUARTER, HALF)
-        nc.vector.tensor_copy(woven(res_bf[0]), planes(acc[:], PACK))
+        acc_a = second(0, 0, 2, "y_acc0_0")
+        acc_b = second(0, 2, 4, "y_acc0_1")
         quantise_z(1)
-        nc.scalar.copy(res[0][:], acc[:])
+        acc_c = second(1, 0, 2, "out_low")
+        acc_d = second(1, 2, 4, "out_high")
+        nc.vector.tensor_copy(plane(res[0], 0, 2), acc_a[:])
+        nc.scalar.copy(plane(res[0], 2, 4), acc_b[:])
         store_rows(nc.sync, 0, 0, PACK)
-        quantise_res(0)
-        acc_a = second(1, 0, 2)
-        acc_b = second(1, 2, 4)
-        nc.vector.tensor_copy(woven(res_bf[1])[:, :, 0:2], planes(acc_a[:], 2))
-        nc.scalar.copy(woven(res_bf[1])[:, :, 2:4], planes(acc_b[:], 2))
-        nc.vector.tensor_copy(plane(res[1], 0, 2), acc_a[:])
+        nc.vector.tensor_copy(woven(res_bf[0])[:, :, 0:2], planes(acc_a[:], 2))
+        nc.scalar.copy(woven(res_bf[0])[:, :, 2:4], planes(acc_b[:], 2))
+        nc.vector.tensor_copy(woven(res_bf[1])[:, :, 0:2], planes(acc_c[:], 2))
+        nc.scalar.copy(woven(res_bf[1])[:, :, 2:4], planes(acc_d[:], 2))
+        nc.vector.tensor_copy(plane(res[1], 0, 2), acc_c[:])
         store_rows(nc.sync, 1, 0, 2)
-        nc.scalar.copy(plane(res[1], 2, 4), acc_b[:])
+        nc.scalar.copy(plane(res[1], 2, 4), acc_d[:])
         store_rows(nc.scalar, 1, 2, 4)
+        quantise_res(0)
         quantise_res(1)
         nc.sync.dma_start(out_words, res_code[:].bitcast(I32))
         for q in range(QUADS):

@@ -142,7 +142,7 @@ def tile_picked_csketch_silu_po_kernel(
             first(acc[:], t, slice(0, S))
             nc.scalar.copy(y[t][:], acc[:])
 
-        looked = [shared("looked0", PACK * V, F32, "x_scale_table")] + [sb("looked%d" % n, PACK * V, F32) for n in (1, 2)]
+        looked = [shared("looked0", PACK * V, F32, "w1_bf1"), shared("looked1", PACK * V, F32, "x_scale_table"), sb("looked2", PACK * V, F32)]
         capped = [sb("capped%d" % h, PACK * HALF, F32) for h in range(2)]
         median = [sb("median%d" % h, PACK * HALF, F32) for h in range(2)]
         z_bf = [sb("z_bf%d" % h, PACK * HALF, BF16) for h in range(2)]
@@ -244,15 +244,14 @@ def tile_picked_csketch_silu_po_kernel(
         quantise_z(1)
         acc_c = second(1, 0, 2, "out_low")
         acc_d = second(1, 2, 4, "out_high")
-        nc.vector.tensor_copy(plane(res[0], 0, 2), acc_a[:])
+        nc.scalar.copy(plane(res[0], 0, 2), acc_a[:])
         nc.scalar.copy(plane(res[0], 2, 4), acc_b[:])
         store_rows(nc.sync, 0, 0, PACK)
-        nc.vector.tensor_copy(woven(res_bf[0])[:, :, 0:2], planes(acc_a[:], 2))
-        nc.scalar.copy(woven(res_bf[0])[:, :, 2:4], planes(acc_b[:], 2))
-        nc.vector.tensor_copy(woven(res_bf[1])[:, :, 0:2], planes(acc_c[:], 2))
-        nc.scalar.copy(woven(res_bf[1])[:, :, 2:4], planes(acc_d[:], 2))
         nc.vector.tensor_copy(plane(res[1], 0, 2), acc_c[:])
         store_rows(nc.sync, 1, 0, 2)
+        nc.vector.tensor_copy(woven(res_bf[0]), planes(res[0][:], PACK))
+        nc.vector.tensor_copy(woven(res_bf[1])[:, :, 0:2], planes(plane(res[1], 0, 2), 2))
+        nc.scalar.copy(woven(res_bf[1])[:, :, 2:4], planes(acc_d[:], 2))
         nc.scalar.copy(plane(res[1], 2, 4), acc_d[:])
         store_rows(nc.scalar, 1, 2, 4)
         quantise_res(0)

@@ -148,7 +148,7 @@ def tile_picked_csketch_silu_po_kernel(
         z_bf = [sb("z_bf%d" % h, PACK * HALF, BF16) for h in range(2)]
         z_code = [sb("z_code%d" % h, HALF, U32) for h in range(2)]
         z_scale = [sb("z_scale%d" % h, HALF, U8) for h in range(2)]
-        res = [sb("res%d" % h, PACK * HALF, F32) for h in range(2)]
+        res = sb("res", PACK * V, F32)
         res_bf = [sb("res_bf%d" % h, PACK * HALF, BF16) for h in range(2)]
         res_code = sb("res_code", V, U32)
         res_scale = sb("res_scale", V, U8)
@@ -211,11 +211,17 @@ def tile_picked_csketch_silu_po_kernel(
                 )
             return acc
 
-        def store_rows(queue, h, t0, t1):
-            queue.dma_start(
-                out_rows[:, t0:t1, h * HALF : (h + 1) * HALF],
-                plane(res[h], t0, t1).rearrange("p (t v) -> p t v", v=HALF),
-            )
+        def results(t0, t1, k0, k1):
+            return res[:].rearrange("p (t v) -> p t v", t=PACK)[:, t0:t1, k0:k1]
+
+        def by_four(ap):
+            return ap.rearrange("p t (c i) -> p c t i", i=4)
+
+        def empty(engine_copy, acc, t0, k0):
+            engine_copy(results(t0, t0 + 2, k0, k0 + HALF), acc[:].rearrange("p (t v) -> p t v", t=2))
+
+        def store_rows(queue, t0, k0, k1):
+            queue.dma_start(out_rows[:, t0 : t0 + 2, k0:k1], results(t0, t0 + 2, k0, k1))
 
         def quantise_res(h):
             cols = slice(h * HALF, (h + 1) * HALF)
@@ -239,21 +245,21 @@ def tile_picked_csketch_silu_po_kernel(
             mid(1, lo, k0, k0 + QUARTER)
             silu(1, k0, k0 + QUARTER)
         quantise_z(0)
-        acc_a = second(0, 0, 2, "y_acc0_0")
-        acc_b = second(0, 2, 4, "y_acc0_1")
+        first_high = second(0, 2, 4, "y_acc0_0")
+        first_low = second(0, 0, 2, "y_acc0_1")
         quantise_z(1)
-        acc_c = second(1, 0, 2, "out_low")
-        acc_d = second(1, 2, 4, "out_high")
-        nc.scalar.copy(plane(res[0], 0, 2), acc_a[:])
-        nc.scalar.copy(plane(res[0], 2, 4), acc_b[:])
-        store_rows(nc.sync, 0, 0, PACK)
-        nc.vector.tensor_copy(plane(res[1], 0, 2), acc_c[:])
-        store_rows(nc.sync, 1, 0, 2)
-        nc.vector.tensor_copy(woven(res_bf[0]), planes(res[0][:], PACK))
-        nc.vector.tensor_copy(woven(res_bf[1])[:, :, 0:2], planes(plane(res[1], 0, 2), 2))
-        nc.scalar.copy(woven(res_bf[1])[:, :, 2:4], planes(acc_d[:], 2))
-        nc.scalar.copy(plane(res[1], 2, 4), acc_d[:])
-        store_rows(nc.scalar, 1, 2, 4)
+        last_low = second(1, 0, 2, "out_low")
+        last_high = second(1, 2, 4, "out_high")
+        empty(nc.scalar.copy, first_high, 2, 0)
+        store_rows(nc.sync, 2, 0, HALF)
+        empty(nc.scalar.copy, first_low, 0, 0)
+        empty(nc.vector.tensor_copy, last_low, 0, HALF)
+        store_rows(nc.sync, 0, 0, V)
+        nc.vector.tensor_copy(woven(res_bf[0]), by_four(results(0, PACK, 0, HALF)))
+        nc.vector.tensor_copy(woven(res_bf[1])[:, :, 0:2], by_four(results(0, 2, HALF, V)))
+        nc.scalar.copy(woven(res_bf[1])[:, :, 2:4], planes(last_high[:], 2))
+        empty(nc.scalar.copy, last_high, 2, HALF)
+        store_rows(nc.scalar, 2, HALF, V)
         quantise_res(0)
         quantise_res(1)
         nc.sync.dma_start(out_words, res_code[:].bitcast(I32))

@@ -89,17 +89,18 @@ def tile_picked_csketch_silu_po_kernel(
         nc.scalar.copy(w1_dst[0][:, :, :, 0:2], w1_src[0][:, :, 0:2, :])
         nc.scalar.copy(w1_dst[1][:, :, :, 0:2], w1_src[0][:, :, 2:4, :])
         sign_rows = [sg.rearrange("(p t) v -> p (t v)", t=PACK) for sg in (sg1, sg2, sg3)]
-        early_signs = shared("early_signs", PACK * V, F32, "w1_raw0")
+        early_signs = shared("early_signs", 2 * V, F32, "w1_raw0")
         for n in range(2):
-            nc.sync.dma_start(early_signs[:, n * 2 * V : (n + 1) * 2 * V], sign_rows[n][:, : 2 * V])
+            nc.sync.dma_start(early_signs[:, n * V : (n + 1) * V], sign_rows[n][:, :V])
         x_word = sb("x_word", S, U32)
         nc.vector.tensor_copy(x_word[:], x_word_table[:].bitcast(U32).indirect(offs_sb[:]))
-        late_signs = shared("late_signs", PACK * V, F32, "x_word_table")
+        late_signs = shared("late_signs", 2 * 3 * V, F32, "x_word_table")
         for n in range(2):
-            nc.sync.dma_start(late_signs[:, n * 2 * V : (n + 1) * 2 * V], sign_rows[n][:, 2 * V :])
+            nc.sync.dma_start(late_signs[:, n * 3 * V : (n + 1) * 3 * V], sign_rows[n][:, V:])
 
-        nc.vector.tensor_copy(w1_dst[0][:, :96, :, 2:4], w1_src[1][:, :96, 0:2, :])
-        nc.scalar.copy(w1_dst[0][:, 96:, :, 2:4], w1_src[1][:, 96:, 0:2, :])
+        for t in range(2):
+            nc.vector.tensor_copy(w1_dst[0][:, :80, t, 2:4], w1_src[1][:, :80, t, :])
+            nc.scalar.copy(w1_dst[0][:, 80:, t, 2:4], w1_src[1][:, 80:, t, :])
         nc.scalar.copy(w1_dst[1][:, :, :, 2:4], w1_src[1][:, :, 2:4, :])
         third_signs = shared("third_signs", PACK * V, F32, "w1_raw1")
         nc.sync.dma_start(third_signs[:], sign_rows[2])
@@ -162,9 +163,10 @@ def tile_picked_csketch_silu_po_kernel(
             cols = slice(t * V, (t + 1) * V)
             if n == 2:
                 sign = third_signs[:, cols]
+            elif t == 0:
+                sign = early_signs[:, n * V : (n + 1) * V]
             else:
-                start = (2 * n + t % 2) * V
-                sign = (early_signs if t < 2 else late_signs)[:, start : start + V]
+                sign = late_signs[:, (3 * n + t - 1) * V : (3 * n + t) * V]
             nc.vector.tensor_tensor(looked[n][:, cols], y[t][:].indirect(hash_sb[n][:]), sign, ALU.mult)
 
         def keys(tile, k0, k1):
@@ -193,8 +195,12 @@ def tile_picked_csketch_silu_po_kernel(
             groups = slice(k0 // 4, k1 // 4)
             nc.scalar.activation(woven(z_bf[h])[:, groups], planes(median[h][:], PACK)[:, groups], SILU)
 
-        def quantise_z(h):
-            nc.vector.quantize_mx(out=z_code[h][:].bitcast(FP8X4), scales=z_scale[h][:], in_=z_bf[h][:])
+        def quantise_z(h, k0, k1):
+            nc.vector.quantize_mx(
+                out=z_code[h][:, k0:k1].bitcast(FP8X4),
+                scales=z_scale[h][:, k0:k1],
+                in_=z_bf[h][:, PACK * k0 : PACK * k1],
+            )
 
         def second(h, t0, t1, tag):
             acc = psum.tile([P, (t1 - t0) * HALF], F32, name="out_acc%d_%d" % (h, t0), tag=tag)
@@ -244,10 +250,11 @@ def tile_picked_csketch_silu_po_kernel(
         for k0 in (0, QUARTER):
             mid(1, lo, k0, k0 + QUARTER)
             silu(1, k0, k0 + QUARTER)
-        quantise_z(0)
+        quantise_z(0, 0, HALF)
         first_high = second(0, 2, 4, "y_acc0_0")
         first_low = second(0, 0, 2, "y_acc0_1")
-        quantise_z(1)
+        quantise_z(1, 0, QUARTER)
+        quantise_z(1, QUARTER, HALF)
         last_low = second(1, 0, 2, "out_low")
         last_high = second(1, 2, 4, "out_high")
         empty(nc.scalar.copy, first_high, 2, 0)

@@ -259,11 +259,12 @@ def tile_picked_csketch_silu_po_kernel(
         last_high = second(1, 2, 4, "out_high")
         empty(nc.scalar.copy, first_high, 2, 0)
         store_rows(nc.sync, 2, 0, HALF)
-        empty(nc.scalar.copy, first_low, 0, 0)
+        nc.scalar.copy(woven(res_bf[0])[:, :, 2:4], planes(first_high[:], 2))
+        empty(nc.vector.tensor_copy, first_low, 0, 0)
         empty(nc.vector.tensor_copy, last_low, 0, HALF)
         store_rows(nc.sync, 0, 0, V)
-        nc.vector.tensor_copy(woven(res_bf[0]), by_four(results(0, PACK, 0, HALF)))
-        nc.vector.tensor_copy(woven(res_bf[1])[:, :, 0:2], by_four(results(0, 2, HALF, V)))
+        for h in range(2):
+            nc.vector.tensor_copy(woven(res_bf[h])[:, :, 0:2], by_four(results(0, 2, h * HALF, (h + 1) * HALF)))
         nc.scalar.copy(woven(res_bf[1])[:, :, 2:4], planes(last_high[:], 2))
         empty(nc.scalar.copy, last_high, 2, HALF)
         store_rows(nc.scalar, 2, HALF, V)

@@ -14,6 +14,7 @@ U8 = mybir.dt.uint8
 FP8X4 = mybir.dt.float8_e4m3fn_x4
 ALU = mybir.AluOpType
 SILU = mybir.ActivationFunctionType.Silu
+COPY = mybir.ActivationFunctionType.Copy
 
 P = 128
 PACK = 4
@@ -50,7 +51,8 @@ def tile_picked_csketch_silu_po_kernel(
         x_scale_table = shared("x_scale_table", T, U8, "x_scale_table")
         w2_scale_raw = sb("w2_scale_raw", N, U8)
         x_scale = sb("x_scale", S, U8)
-        for tile in (x_scale_table, w2_scale_raw, x_scale):
+        w2_scale = sb("w2_scale", N, U8)
+        for tile in (x_scale_table, w2_scale_raw, x_scale, w2_scale):
             nc.vector.memset(words(tile[:]), 0)
         warm_in = sb("warm_in", 8, F32)
         warm_out = sb("warm_out", 8, F32)
@@ -69,12 +71,15 @@ def tile_picked_csketch_silu_po_kernel(
         nc.sync.dma_start(w1_raw[1][:], w1_rows[:, 2 * H :])
         for tile, h in zip(hash_sb[1:], (h2, h3)):
             nc.sync.dma_start(tile[:], h)
+        sign_rows = [sg.rearrange("(p t) v -> p (t v)", t=PACK) for sg in (sg1, sg2, sg3)]
 
         x_scale_spread = sb("x_scale_spread", S, U8)
         nc.vector.tensor_copy(x_scale_spread[:], x_scale_table[:].indirect(offs_sb[:]))
         place_scale_rows(x_scale, x_scale_spread)
-        w2_word_raw = shared("w2_word_raw", N, I32, "x_scale_table")
-        nc.sync.dma_start(w2_word_raw[:], words(w2_words[0].rearrange("p c r -> p (c r)")))
+        first_signs = shared("first_signs", PACK * V, F32, "x_scale_table")
+        for a in range(2):
+            cols = slice(2 * a * V, 2 * (a + 1) * V)
+            nc.sync.dma_start(first_signs[:, cols], sign_rows[0][:, cols])
         w2_scale_spread = sb("w2_scale_spread", N, U8)
         nc.vector.tensor_copy(
             w2_scale_spread[:].rearrange("p (t c i) -> p c t i", t=PACK, i=16),
@@ -88,22 +93,20 @@ def tile_picked_csketch_silu_po_kernel(
         w1_dst = [tile[:].rearrange("p (t m j) -> p m t j", t=2, j=PACK) for tile in w1_bf]
         nc.scalar.copy(w1_dst[0][:, :, :, 0:2], w1_src[0][:, :, 0:2, :])
         nc.scalar.copy(w1_dst[1][:, :, :, 0:2], w1_src[0][:, :, 2:4, :])
-        sign_rows = [sg.rearrange("(p t) v -> p (t v)", t=PACK) for sg in (sg1, sg2, sg3)]
-        early_signs = shared("early_signs", 2 * V, F32, "w1_raw0")
-        for n in range(2):
-            nc.sync.dma_start(early_signs[:, n * V : (n + 1) * V], sign_rows[n][:, :V])
+        second_signs = shared("second_signs", PACK * V, F32, "w1_raw0")
+        nc.sync.dma_start(second_signs[:], sign_rows[1])
+        place_scale_rows(w2_scale, w2_scale_spread)
         x_word = sb("x_word", S, U32)
         nc.vector.tensor_copy(x_word[:], x_word_table[:].bitcast(U32).indirect(offs_sb[:]))
-        late_signs = shared("late_signs", 2 * 3 * V, F32, "x_word_table")
-        for n in range(2):
-            nc.sync.dma_start(late_signs[:, n * 3 * V : (n + 1) * 3 * V], sign_rows[n][:, V:])
+        third_signs = shared("third_signs", PACK * V, F32, "x_word_table")
+        nc.sync.dma_start(third_signs[:], sign_rows[2])
 
         for t in range(2):
             nc.vector.tensor_copy(w1_dst[0][:, :80, t, 2:4], w1_src[1][:, :80, t, :])
             nc.scalar.copy(w1_dst[0][:, 80:, t, 2:4], w1_src[1][:, 80:, t, :])
         nc.scalar.copy(w1_dst[1][:, :, :, 2:4], w1_src[1][:, :, 2:4, :])
-        third_signs = shared("third_signs", PACK * V, F32, "w1_raw1")
-        nc.sync.dma_start(third_signs[:], sign_rows[2])
+        w2_word_raw = shared("w2_word_raw", N, I32, "w1_raw1")
+        nc.sync.dma_start(w2_word_raw[:], words(w2_words[0].rearrange("p c r -> p (c r)")))
         for t in range(2):
             nc.vector.quantize_mx(
                 out=w1_code[0][:, t * P : (t + 1) * P].bitcast(FP8X4),
@@ -112,14 +115,6 @@ def tile_picked_csketch_silu_po_kernel(
             )
         w1_code.append(sb("w1_code1", 2 * P, U32))
         nc.vector.quantize_mx(out=w1_code[1][:].bitcast(FP8X4), scales=w1_scale[1][:], in_=w1_bf[1][:])
-        w2_word = sb("w2_word", N, I32)
-        nc.vector.tensor_copy(
-            w2_word[:].rearrange("p (t c i) -> p c t i", t=PACK, i=4),
-            w2_word_raw[:].rearrange("p (c i t) -> p c t i", t=PACK, i=4),
-        )
-        w2_scale = shared("w2_scale", N, U8, "w1_bf0")
-        nc.vector.memset(words(w2_scale[:]), 0)
-        place_scale_rows(w2_scale, w2_scale_spread)
         y = [keep.tile([P, S], F32, name="y%d" % t, tag="y%d" % t, align_bytes=64) for t in range(PACK)]
 
         def first(acc, t, cols):
@@ -137,14 +132,17 @@ def tile_picked_csketch_silu_po_kernel(
         for a in range(2):
             acc = psum.tile([P, S // 2], F32, name="y_acc0_%d" % a, tag="y_acc0_%d" % a)
             first(acc[:], 0, slice(a * 256, (a + 1) * 256))
-            nc.scalar.copy(y[0][:, a * 256 : (a + 1) * 256], acc[:])
+            (nc.vector.tensor_copy, nc.scalar.copy)[a](y[0][:, a * 256 : (a + 1) * 256], acc[:])
         for t in range(1, PACK):
             acc = psum.tile([P, S], F32, name="y_acc%d" % t)
             first(acc[:], t, slice(0, S))
             nc.scalar.copy(y[t][:], acc[:])
 
-        looked = [shared("looked0", PACK * V, F32, "w1_bf1"), shared("looked1", PACK * V, F32, "x_scale_table"), sb("looked2", PACK * V, F32)]
-        capped = [sb("capped%d" % h, PACK * HALF, F32) for h in range(2)]
+        looked = [shared("looked0", PACK * V, F32, "w1_bf1"), sb("looked1", PACK * V, F32), sb("looked2", PACK * V, F32)]
+        plain = [sb("plain%d" % n, PACK * V, F32) for n in (1, 2)]
+        hi = sb("hi", PACK * V, F32)
+        lo = sb("lo", PACK * V, F32)
+        capped = sb("capped", PACK * V, F32)
         median = [sb("median%d" % h, PACK * HALF, F32) for h in range(2)]
         z_bf = [sb("z_bf%d" % h, PACK * HALF, BF16) for h in range(2)]
         z_code = [sb("z_code%d" % h, HALF, U32) for h in range(2)]
@@ -156,34 +154,27 @@ def tile_picked_csketch_silu_po_kernel(
         out_rows = out_0.rearrange("(p t) v -> p t v", t=PACK)
         out_words = out_1[0].rearrange("p c r -> p (c r)").bitcast(I32)
 
-        def plane(tile, t0, t1):
-            return tile[:, t0 * HALF : t1 * HALF]
-
-        def look(n, t):
+        def look_signed(t):
             cols = slice(t * V, (t + 1) * V)
-            if n == 2:
-                sign = third_signs[:, cols]
-            elif t == 0:
-                sign = early_signs[:, n * V : (n + 1) * V]
-            else:
-                sign = late_signs[:, (3 * n + t - 1) * V : (3 * n + t) * V]
-            nc.vector.tensor_tensor(looked[n][:, cols], y[t][:].indirect(hash_sb[n][:]), sign, ALU.mult)
+            nc.vector.tensor_tensor(looked[0][:, cols], y[t][:].indirect(hash_sb[0][:]), first_signs[:, cols], ALU.mult)
+
+        def look_plain(n, t):
+            nc.scalar.activation(plain[n - 1][:, t * V : (t + 1) * V], y[t][:].indirect(hash_sb[n][:]), COPY)
 
         def keys(tile, k0, k1):
             return tile[:].rearrange("p (t v) -> p t v", t=PACK)[:, :, k0:k1]
 
-        def bound(name, tag, op):
-            tile = keep.tile([P, PACK * V], F32, name=name, tag=tag, align_bytes=64)
-            nc.vector.tensor_tensor(tile[:], looked[0][:], looked[1][:], op)
-            return tile
+        def on_planes(op, out, in0, in1, t0, t1):
+            cols = slice(t0 * V, t1 * V)
+            nc.vector.tensor_tensor(out[:, cols], in0[:, cols], in1[:, cols], op)
 
-        def cap(h, hi, k0, k1):
-            high, third = [keys(tile, h * HALF + k0, h * HALF + k1) for tile in (hi, looked[2])]
-            nc.vector.tensor_tensor(keys(capped[h], k0, k1), high, third, ALU.min)
+        def bounds(t0, t1):
+            on_planes(ALU.max, hi, looked[0], looked[1], t0, t1)
+            on_planes(ALU.min, lo, looked[0], looked[1], t0, t1)
 
-        def mid(h, lo, k0, k1):
-            low = keys(lo, h * HALF + k0, h * HALF + k1)
-            nc.vector.tensor_tensor(keys(median[h], k0, k1), low, keys(capped[h], k0, k1), ALU.max)
+        def mid(h, k0, k1):
+            low, high = [keys(tile, h * HALF + k0, h * HALF + k1) for tile in (lo, capped)]
+            nc.vector.tensor_tensor(keys(median[h], k0, k1), low, high, ALU.max)
 
         def woven(tile):
             return tile[:].rearrange("p (c i t) -> p c t i", t=PACK, i=4)
@@ -234,21 +225,31 @@ def tile_picked_csketch_silu_po_kernel(
             nc.vector.quantize_mx(out=res_code[:, cols].bitcast(FP8X4), scales=res_scale[:, cols], in_=res_bf[h][:])
 
         for t in range(PACK):
-            for n in range(2):
-                look(n, t)
-        look(2, 0)
-        look(2, 1)
-        hi = bound("hi", "y0", ALU.max)
-        look(2, 2)
-        look(2, 3)
-        lo = bound("lo", "y2", ALU.min)
-        cap(0, hi, 0, HALF)
-        cap(1, hi, 0, QUARTER)
-        mid(0, lo, 0, HALF)
+            look_signed(t)
+        for n in (1, 2):
+            for t in range(PACK):
+                look_plain(n, t)
+        w2_word = sb("w2_word", N, U32)
+        nc.scalar.copy(
+            w2_word[:].rearrange("p (t c i) -> p c t i", t=PACK, i=4),
+            w2_word_raw[:].bitcast(U32).rearrange("p (c i t) -> p c t i", t=PACK, i=4),
+        )
+        on_planes(ALU.mult, looked[1], plain[0], second_signs, 0, 1)
+        on_planes(ALU.mult, looked[1], plain[0], second_signs, 1, 2)
+        bounds(0, 1)
+        on_planes(ALU.mult, looked[1], plain[0], second_signs, 2, 3)
+        bounds(1, 2)
+        on_planes(ALU.mult, looked[1], plain[0], second_signs, 3, 4)
+        on_planes(ALU.mult, looked[2], plain[1], third_signs, 0, 1)
+        bounds(2, 4)
+        on_planes(ALU.mult, looked[2], plain[1], third_signs, 1, 3)
+        on_planes(ALU.mult, looked[2], plain[1], third_signs, 3, 4)
+        on_planes(ALU.min, capped, hi, looked[2], 0, 2)
+        on_planes(ALU.min, capped, hi, looked[2], 2, 4)
+        mid(0, 0, HALF)
         silu(0, 0, HALF)
-        cap(1, hi, QUARTER, HALF)
         for k0 in (0, QUARTER):
-            mid(1, lo, k0, k0 + QUARTER)
+            mid(1, k0, k0 + QUARTER)
             silu(1, k0, k0 + QUARTER)
         quantise_z(0, 0, HALF)
         first_high = second(0, 2, 4, "y_acc0_0")

@@ -76,10 +76,12 @@ def tile_picked_csketch_silu_po_kernel(
         x_scale_spread = sb("x_scale_spread", S, U8)
         nc.vector.tensor_copy(x_scale_spread[:], x_scale_table[:].indirect(offs_sb[:]))
         place_scale_rows(x_scale, x_scale_spread)
-        first_signs = shared("first_signs", PACK * V, F32, "x_scale_table")
+        early_signs = shared("early_signs", 2 * PACK * V, F32, "x_scale_table")
+        first_signs, second_signs = early_signs[:, : PACK * V], early_signs[:, PACK * V :]
         for a in range(2):
             cols = slice(2 * a * V, 2 * (a + 1) * V)
             nc.sync.dma_start(first_signs[:, cols], sign_rows[0][:, cols])
+        nc.sync.dma_start(second_signs, sign_rows[1])
         w2_scale_spread = sb("w2_scale_spread", N, U8)
         nc.vector.tensor_copy(
             w2_scale_spread[:].rearrange("p (t c i) -> p c t i", t=PACK, i=16),
@@ -93,8 +95,6 @@ def tile_picked_csketch_silu_po_kernel(
         w1_dst = [tile[:].rearrange("p (t m j) -> p m t j", t=2, j=PACK) for tile in w1_bf]
         nc.scalar.copy(w1_dst[0][:, :, :, 0:2], w1_src[0][:, :, 0:2, :])
         nc.scalar.copy(w1_dst[1][:, :, :, 0:2], w1_src[0][:, :, 2:4, :])
-        second_signs = shared("second_signs", PACK * V, F32, "w1_raw0")
-        nc.sync.dma_start(second_signs[:], sign_rows[1])
         place_scale_rows(w2_scale, w2_scale_spread)
         x_word = sb("x_word", S, U32)
         nc.vector.tensor_copy(x_word[:], x_word_table[:].bitcast(U32).indirect(offs_sb[:]))
@@ -129,14 +129,13 @@ def tile_picked_csketch_silu_po_kernel(
                 stop=True,
             )
 
-        for a in range(2):
-            acc = psum.tile([P, S // 2], F32, name="y_acc0_%d" % a, tag="y_acc0_%d" % a)
-            first(acc[:], 0, slice(a * 256, (a + 1) * 256))
-            (nc.vector.tensor_copy, nc.scalar.copy)[a](y[0][:, a * 256 : (a + 1) * 256], acc[:])
-        for t in range(1, PACK):
-            acc = psum.tile([P, S], F32, name="y_acc%d" % t)
-            first(acc[:], t, slice(0, S))
-            nc.scalar.copy(y[t][:], acc[:])
+        for t in range(PACK):
+            for a in range(2):
+                cols = slice(a * S // 2, (a + 1) * S // 2)
+                acc = psum.tile([P, S // 2], F32, name="y_acc%d_%d" % (t, a), tag="bank%d" % (2 * t + a))
+                first(acc[:], t, cols)
+                engine_copy = nc.vector.tensor_copy if (t, a) == (0, 0) else nc.scalar.copy
+                engine_copy(y[t][:, cols], acc[:])
 
         looked = [shared("looked0", PACK * V, F32, "w1_bf1"), sb("looked1", PACK * V, F32), sb("looked2", PACK * V, F32)]
         plain = [sb("plain%d" % n, PACK * V, F32) for n in (1, 2)]
@@ -158,8 +157,9 @@ def tile_picked_csketch_silu_po_kernel(
             cols = slice(t * V, (t + 1) * V)
             nc.vector.tensor_tensor(looked[0][:, cols], y[t][:].indirect(hash_sb[0][:]), first_signs[:, cols], ALU.mult)
 
-        def look_plain(n, t):
-            nc.scalar.activation(plain[n - 1][:, t * V : (t + 1) * V], y[t][:].indirect(hash_sb[n][:]), COPY)
+        def look_plain(n, t, k0, k1):
+            picked = y[t][:].indirect(hash_sb[n][:, k0 // 16 : k1 // 16])
+            nc.scalar.activation(plain[n - 1][:, t * V + k0 : t * V + k1], picked, COPY)
 
         def keys(tile, k0, k1):
             return tile[:].rearrange("p (t v) -> p t v", t=PACK)[:, :, k0:k1]
@@ -168,9 +168,8 @@ def tile_picked_csketch_silu_po_kernel(
             cols = slice(t0 * V, t1 * V)
             nc.vector.tensor_tensor(out[:, cols], in0[:, cols], in1[:, cols], op)
 
-        def bounds(t0, t1):
-            on_planes(ALU.max, hi, looked[0], looked[1], t0, t1)
-            on_planes(ALU.min, lo, looked[0], looked[1], t0, t1)
+        def on_keys(op, out, in0, in1, k0, k1):
+            nc.vector.tensor_tensor(keys(out, k0, k1), keys(in0, k0, k1), keys(in1, k0, k1), op)
 
         def mid(h, k0, k1):
             low, high = [keys(tile, h * HALF + k0, h * HALF + k1) for tile in (lo, capped)]
@@ -226,9 +225,11 @@ def tile_picked_csketch_silu_po_kernel(
 
         for t in range(PACK):
             look_signed(t)
-        for n in (1, 2):
+        for t in range(PACK):
+            look_plain(1, t, 0, V)
+        for h in range(2):
             for t in range(PACK):
-                look_plain(n, t)
+                look_plain(2, t, h * HALF, (h + 1) * HALF)
         w2_word = sb("w2_word", N, U32)
         nc.scalar.copy(
             w2_word[:].rearrange("p (t c i) -> p c t i", t=PACK, i=4),
@@ -236,28 +237,31 @@ def tile_picked_csketch_silu_po_kernel(
         )
         on_planes(ALU.mult, looked[1], plain[0], second_signs, 0, 1)
         on_planes(ALU.mult, looked[1], plain[0], second_signs, 1, 2)
-        bounds(0, 1)
+        on_planes(ALU.max, hi, looked[0], looked[1], 0, 1)
         on_planes(ALU.mult, looked[1], plain[0], second_signs, 2, 3)
-        bounds(1, 2)
+        on_planes(ALU.min, lo, looked[0], looked[1], 0, 2)
         on_planes(ALU.mult, looked[1], plain[0], second_signs, 3, 4)
-        on_planes(ALU.mult, looked[2], plain[1], third_signs, 0, 1)
-        bounds(2, 4)
-        on_planes(ALU.mult, looked[2], plain[1], third_signs, 1, 3)
-        on_planes(ALU.mult, looked[2], plain[1], third_signs, 3, 4)
-        on_planes(ALU.min, capped, hi, looked[2], 0, 2)
-        on_planes(ALU.min, capped, hi, looked[2], 2, 4)
+        on_planes(ALU.max, hi, looked[0], looked[1], 1, 3)
+        on_planes(ALU.max, hi, looked[0], looked[1], 3, 4)
+        on_keys(ALU.mult, looked[2], plain[1], third_signs, 0, HALF)
+        on_planes(ALU.min, lo, looked[0], looked[1], 2, 4)
+        on_keys(ALU.min, capped, hi, looked[2], 0, HALF)
+        on_keys(ALU.mult, looked[2], plain[1], third_signs, HALF, V)
         mid(0, 0, HALF)
         silu(0, 0, HALF)
-        for k0 in (0, QUARTER):
-            mid(1, k0, k0 + QUARTER)
-            silu(1, k0, k0 + QUARTER)
+        for k0 in (HALF, HALF + QUARTER):
+            on_keys(ALU.min, capped, hi, looked[2], k0, k0 + QUARTER)
+        mid(1, 0, QUARTER)
+        silu(1, 0, QUARTER)
         quantise_z(0, 0, HALF)
-        first_high = second(0, 2, 4, "y_acc0_0")
-        first_low = second(0, 0, 2, "y_acc0_1")
+        mid(1, QUARTER, HALF)
+        silu(1, QUARTER, HALF)
+        first_high = second(0, 2, 4, "bank0")
+        first_low = second(0, 0, 2, "bank1")
         quantise_z(1, 0, QUARTER)
         quantise_z(1, QUARTER, HALF)
-        last_low = second(1, 0, 2, "out_low")
-        last_high = second(1, 2, 4, "out_high")
+        last_low = second(1, 0, 2, "bank2")
+        last_high = second(1, 2, 4, "bank3")
         empty(nc.scalar.copy, first_high, 2, 0)
         store_rows(nc.sync, 2, 0, HALF)
         nc.scalar.copy(woven(res_bf[0])[:, :, 2:4], planes(first_high[:], 2))

@@ -76,12 +76,13 @@ def tile_picked_csketch_silu_po_kernel(
         x_scale_spread = sb("x_scale_spread", S, U8)
         nc.vector.tensor_copy(x_scale_spread[:], x_scale_table[:].indirect(offs_sb[:]))
         place_scale_rows(x_scale, x_scale_spread)
-        early_signs = shared("early_signs", 2 * PACK * V, F32, "x_scale_table")
-        first_signs, second_signs = early_signs[:, : PACK * V], early_signs[:, PACK * V :]
+        signs = shared("signs", 3 * PACK * V, F32, "x_scale_table")
+        first_signs, second_signs, third_signs = [signs[:, n * PACK * V : (n + 1) * PACK * V] for n in range(3)]
         for a in range(2):
             cols = slice(2 * a * V, 2 * (a + 1) * V)
             nc.sync.dma_start(first_signs[:, cols], sign_rows[0][:, cols])
         nc.sync.dma_start(second_signs, sign_rows[1])
+        nc.sync.dma_start(third_signs, sign_rows[2])
         w2_scale_spread = sb("w2_scale_spread", N, U8)
         nc.vector.tensor_copy(
             w2_scale_spread[:].rearrange("p (t c i) -> p c t i", t=PACK, i=16),
@@ -98,8 +99,6 @@ def tile_picked_csketch_silu_po_kernel(
         place_scale_rows(w2_scale, w2_scale_spread)
         x_word = sb("x_word", S, U32)
         nc.vector.tensor_copy(x_word[:], x_word_table[:].bitcast(U32).indirect(offs_sb[:]))
-        third_signs = shared("third_signs", PACK * V, F32, "x_word_table")
-        nc.sync.dma_start(third_signs[:], sign_rows[2])
 
         for t in range(2):
             nc.vector.tensor_copy(w1_dst[0][:, :80, t, 2:4], w1_src[1][:, :80, t, :])
@@ -115,7 +114,7 @@ def tile_picked_csketch_silu_po_kernel(
             )
         w1_code.append(sb("w1_code1", 2 * P, U32))
         nc.vector.quantize_mx(out=w1_code[1][:].bitcast(FP8X4), scales=w1_scale[1][:], in_=w1_bf[1][:])
-        y = [keep.tile([P, S], F32, name="y%d" % t, tag="y%d" % t, align_bytes=64) for t in range(PACK)]
+        y = [shared("y%d" % t, S, F32, "y%d" % t) for t in range(PACK)]
 
         def first(acc, t, cols):
             rows = slice(t % 2 * P, (t % 2 + 1) * P)
@@ -137,16 +136,17 @@ def tile_picked_csketch_silu_po_kernel(
                 engine_copy = nc.vector.tensor_copy if (t, a) == (0, 0) else nc.scalar.copy
                 engine_copy(y[t][:, cols], acc[:])
 
-        looked = [shared("looked0", PACK * V, F32, "w1_bf1"), sb("looked1", PACK * V, F32), sb("looked2", PACK * V, F32)]
-        plain = [sb("plain%d" % n, PACK * V, F32) for n in (1, 2)]
+        looked = [shared("looked0", PACK * V, F32, "w1_bf1"), sb("looked1", PACK * V, F32)]
+        second_plain = sb("second_plain", PACK * V, F32)
+        third_plain = [sb("third_plain%d" % h, PACK * HALF, F32) for h in range(2)]
+        third = [sb("third%d" % h, PACK * HALF, F32) for h in range(2)]
         hi = sb("hi", PACK * V, F32)
         lo = sb("lo", PACK * V, F32)
-        capped = sb("capped", PACK * V, F32)
-        median = [sb("median%d" % h, PACK * HALF, F32) for h in range(2)]
+        capped = [sb("capped%d" % h, PACK * HALF, F32) for h in range(2)]
+        median = [shared("median%d" % h, PACK * HALF, F32, "median%d" % h) for h in range(2)]
         z_bf = [sb("z_bf%d" % h, PACK * HALF, BF16) for h in range(2)]
         z_code = [sb("z_code%d" % h, HALF, U32) for h in range(2)]
         z_scale = [sb("z_scale%d" % h, HALF, U8) for h in range(2)]
-        res = sb("res", PACK * V, F32)
         res_bf = [sb("res_bf%d" % h, PACK * HALF, BF16) for h in range(2)]
         res_code = sb("res_code", V, U32)
         res_scale = sb("res_scale", V, U8)
@@ -157,9 +157,9 @@ def tile_picked_csketch_silu_po_kernel(
             cols = slice(t * V, (t + 1) * V)
             nc.vector.tensor_tensor(looked[0][:, cols], y[t][:].indirect(hash_sb[0][:]), first_signs[:, cols], ALU.mult)
 
-        def look_plain(n, t, k0, k1):
+        def look_plain(out, n, t, k0, k1):
             picked = y[t][:].indirect(hash_sb[n][:, k0 // 16 : k1 // 16])
-            nc.scalar.activation(plain[n - 1][:, t * V + k0 : t * V + k1], picked, COPY)
+            nc.scalar.activation(out[:, t * (k1 - k0) : (t + 1) * (k1 - k0)], picked, COPY)
 
         def keys(tile, k0, k1):
             return tile[:].rearrange("p (t v) -> p t v", t=PACK)[:, :, k0:k1]
@@ -168,12 +168,17 @@ def tile_picked_csketch_silu_po_kernel(
             cols = slice(t0 * V, t1 * V)
             nc.vector.tensor_tensor(out[:, cols], in0[:, cols], in1[:, cols], op)
 
-        def on_keys(op, out, in0, in1, k0, k1):
-            nc.vector.tensor_tensor(keys(out, k0, k1), keys(in0, k0, k1), keys(in1, k0, k1), op)
+        def sign_third(h):
+            sign = keys(third_signs, h * HALF, (h + 1) * HALF)
+            nc.vector.tensor_tensor(keys(third[h], 0, HALF), keys(third_plain[h], 0, HALF), sign, ALU.mult)
+
+        def cap(h, k0, k1):
+            high = keys(hi, h * HALF + k0, h * HALF + k1)
+            nc.vector.tensor_tensor(keys(capped[h], k0, k1), high, keys(third[h], k0, k1), ALU.min)
 
         def mid(h, k0, k1):
-            low, high = [keys(tile, h * HALF + k0, h * HALF + k1) for tile in (lo, capped)]
-            nc.vector.tensor_tensor(keys(median[h], k0, k1), low, high, ALU.max)
+            low = keys(lo, h * HALF + k0, h * HALF + k1)
+            nc.vector.tensor_tensor(keys(median[h], k0, k1), low, keys(capped[h], k0, k1), ALU.max)
 
         def woven(tile):
             return tile[:].rearrange("p (c i t) -> p c t i", t=PACK, i=4)
@@ -207,17 +212,9 @@ def tile_picked_csketch_silu_po_kernel(
                 )
             return acc
 
-        def results(t0, t1, k0, k1):
-            return res[:].rearrange("p (t v) -> p t v", t=PACK)[:, t0:t1, k0:k1]
-
-        def by_four(ap):
-            return ap.rearrange("p t (c i) -> p c t i", i=4)
-
-        def empty(engine_copy, acc, t0, k0):
-            engine_copy(results(t0, t0 + 2, k0, k0 + HALF), acc[:].rearrange("p (t v) -> p t v", t=2))
-
-        def store_rows(queue, t0, k0, k1):
-            queue.dma_start(out_rows[:, t0 : t0 + 2, k0:k1], results(t0, t0 + 2, k0, k1))
+        def store_rows(queue, res, t0, t1, h):
+            rows = res[:, t0 * HALF : t1 * HALF].rearrange("p (t v) -> p t v", v=HALF)
+            queue.dma_start(out_rows[:, t0:t1, h * HALF : (h + 1) * HALF], rows)
 
         def quantise_res(h):
             cols = slice(h * HALF, (h + 1) * HALF)
@@ -226,54 +223,55 @@ def tile_picked_csketch_silu_po_kernel(
         for t in range(PACK):
             look_signed(t)
         for t in range(PACK):
-            look_plain(1, t, 0, V)
+            look_plain(second_plain, 1, t, 0, V)
         for h in range(2):
             for t in range(PACK):
-                look_plain(2, t, h * HALF, (h + 1) * HALF)
+                look_plain(third_plain[h], 2, t, h * HALF, (h + 1) * HALF)
         w2_word = sb("w2_word", N, U32)
         nc.scalar.copy(
             w2_word[:].rearrange("p (t c i) -> p c t i", t=PACK, i=4),
             w2_word_raw[:].bitcast(U32).rearrange("p (c i t) -> p c t i", t=PACK, i=4),
         )
-        on_planes(ALU.mult, looked[1], plain[0], second_signs, 0, 1)
-        on_planes(ALU.mult, looked[1], plain[0], second_signs, 1, 2)
+        on_planes(ALU.mult, looked[1], second_plain, second_signs, 0, 1)
+        on_planes(ALU.mult, looked[1], second_plain, second_signs, 1, 2)
         on_planes(ALU.max, hi, looked[0], looked[1], 0, 1)
-        on_planes(ALU.mult, looked[1], plain[0], second_signs, 2, 3)
+        on_planes(ALU.mult, looked[1], second_plain, second_signs, 2, 3)
         on_planes(ALU.min, lo, looked[0], looked[1], 0, 2)
-        on_planes(ALU.mult, looked[1], plain[0], second_signs, 3, 4)
+        on_planes(ALU.mult, looked[1], second_plain, second_signs, 3, 4)
         on_planes(ALU.max, hi, looked[0], looked[1], 1, 3)
         on_planes(ALU.max, hi, looked[0], looked[1], 3, 4)
-        on_keys(ALU.mult, looked[2], plain[1], third_signs, 0, HALF)
+        sign_third(0)
         on_planes(ALU.min, lo, looked[0], looked[1], 2, 4)
-        on_keys(ALU.min, capped, hi, looked[2], 0, HALF)
-        on_keys(ALU.mult, looked[2], plain[1], third_signs, HALF, V)
+        cap(0, 0, HALF)
+        sign_third(1)
         mid(0, 0, HALF)
         silu(0, 0, HALF)
-        for k0 in (HALF, HALF + QUARTER):
-            on_keys(ALU.min, capped, hi, looked[2], k0, k0 + QUARTER)
-        mid(1, 0, QUARTER)
-        silu(1, 0, QUARTER)
+        for k0 in (0, QUARTER):
+            cap(1, k0, k0 + QUARTER)
+        for k0 in (0, QUARTER):
+            mid(1, k0, k0 + QUARTER)
+            silu(1, k0, k0 + QUARTER)
         quantise_z(0, 0, HALF)
-        mid(1, QUARTER, HALF)
-        silu(1, QUARTER, HALF)
-        first_high = second(0, 2, 4, "bank0")
-        first_low = second(0, 0, 2, "bank1")
+        first_low = second(0, 0, 2, "bank0")
+        first_high = second(0, 2, 4, "bank1")
         quantise_z(1, 0, QUARTER)
         quantise_z(1, QUARTER, HALF)
         last_low = second(1, 0, 2, "bank2")
         last_high = second(1, 2, 4, "bank3")
-        empty(nc.scalar.copy, first_high, 2, 0)
-        store_rows(nc.sync, 2, 0, HALF)
-        nc.scalar.copy(woven(res_bf[0])[:, :, 2:4], planes(first_high[:], 2))
-        empty(nc.vector.tensor_copy, first_low, 0, 0)
-        empty(nc.vector.tensor_copy, last_low, 0, HALF)
-        store_rows(nc.sync, 0, 0, V)
-        for h in range(2):
-            nc.vector.tensor_copy(woven(res_bf[h])[:, :, 0:2], by_four(results(0, 2, h * HALF, (h + 1) * HALF)))
-        nc.scalar.copy(woven(res_bf[1])[:, :, 2:4], planes(last_high[:], 2))
-        empty(nc.scalar.copy, last_high, 2, HALF)
-        store_rows(nc.scalar, 2, HALF, V)
+        first_res = shared("first_res", PACK * HALF, F32, "median1")
+        last_res = sb("last_res", PACK * HALF, F32)
+        low, high = slice(0, 2 * HALF), slice(2 * HALF, PACK * HALF)
+        nc.vector.tensor_copy(first_res[:, low], first_low[:])
+        nc.scalar.copy(first_res[:, high], first_high[:])
+        store_rows(nc.sync, first_res, 0, PACK, 0)
+        nc.vector.tensor_copy(last_res[:, low], last_low[:])
+        store_rows(nc.sync, last_res, 0, 2, 1)
+        nc.vector.tensor_copy(woven(res_bf[0]), planes(first_res[:], PACK))
+        nc.vector.tensor_copy(woven(res_bf[1])[:, :, 0:2], planes(last_res[:, low], 2))
         quantise_res(0)
+        nc.scalar.copy(woven(res_bf[1])[:, :, 2:4], planes(last_high[:], 2))
+        nc.scalar.copy(last_res[:, high], last_high[:])
+        store_rows(nc.scalar, last_res, 2, PACK, 1)
         quantise_res(1)
         nc.sync.dma_start(out_words, res_code[:].bitcast(I32))
         for q in range(QUADS):

@@ -21,6 +21,7 @@ PACK = 4
 QUADS = 4
 HALF = V // 2
 QUARTER = V // 4
+EIGHTH = V // 8
 
 
 def tile_picked_csketch_silu_po_kernel(
@@ -238,22 +239,23 @@ def tile_picked_csketch_silu_po_kernel(
         on_planes(ALU.mult, looked[1], second_plain, second_signs, 2, 3)
         on_planes(ALU.min, lo, looked[0], looked[1], 0, 2)
         on_planes(ALU.mult, looked[1], second_plain, second_signs, 3, 4)
-        on_planes(ALU.max, hi, looked[0], looked[1], 1, 3)
-        on_planes(ALU.max, hi, looked[0], looked[1], 3, 4)
+        on_planes(ALU.min, lo, looked[0], looked[1], 2, 3)
+        on_planes(ALU.max, hi, looked[0], looked[1], 1, 4)
         sign_third(0)
-        on_planes(ALU.min, lo, looked[0], looked[1], 2, 4)
+        on_planes(ALU.min, lo, looked[0], looked[1], 3, 4)
         cap(0, 0, HALF)
         sign_third(1)
         mid(0, 0, HALF)
         silu(0, 0, HALF)
         for k0 in (0, QUARTER):
             cap(1, k0, k0 + QUARTER)
-        for k0 in (0, QUARTER):
-            mid(1, k0, k0 + QUARTER)
-            silu(1, k0, k0 + QUARTER)
+        last_pieces = ((0, QUARTER), (QUARTER, QUARTER + EIGHTH), (QUARTER + EIGHTH, HALF))
+        for k0, k1 in last_pieces:
+            mid(1, k0, k1)
+            silu(1, k0, k1)
         quantise_z(0, 0, HALF)
-        first_low = second(0, 0, 2, "bank0")
         first_high = second(0, 2, 4, "bank1")
+        first_low = second(0, 0, 2, "bank0")
         quantise_z(1, 0, QUARTER)
         quantise_z(1, QUARTER, HALF)
         last_low = second(1, 0, 2, "bank2")
@@ -264,11 +266,11 @@ def tile_picked_csketch_silu_po_kernel(
         nc.vector.tensor_copy(first_res[:, low], first_low[:])
         nc.scalar.copy(first_res[:, high], first_high[:])
         store_rows(nc.sync, first_res, 0, PACK, 0)
-        nc.vector.tensor_copy(last_res[:, low], last_low[:])
-        store_rows(nc.sync, last_res, 0, 2, 1)
         nc.vector.tensor_copy(woven(res_bf[0]), planes(first_res[:], PACK))
-        nc.vector.tensor_copy(woven(res_bf[1])[:, :, 0:2], planes(last_res[:, low], 2))
+        nc.scalar.copy(last_res[:, low], last_low[:])
+        store_rows(nc.sync, last_res, 0, 2, 1)
         quantise_res(0)
+        nc.vector.tensor_copy(woven(res_bf[1])[:, :, 0:2], planes(last_res[:, low], 2))
         nc.scalar.copy(woven(res_bf[1])[:, :, 2:4], planes(last_high[:], 2))
         nc.scalar.copy(last_res[:, high], last_high[:])
         store_rows(nc.scalar, last_res, 2, PACK, 1)

@@ -21,7 +21,6 @@ PACK = 4
 QUADS = 4
 HALF = V // 2
 QUARTER = V // 4
-EIGHTH = V // 8
 
 
 def tile_picked_csketch_silu_po_kernel(
@@ -78,12 +77,12 @@ def tile_picked_csketch_silu_po_kernel(
         nc.vector.tensor_copy(x_scale_spread[:], x_scale_table[:].indirect(offs_sb[:]))
         place_scale_rows(x_scale, x_scale_spread)
         signs = shared("signs", 3 * PACK * V, F32, "x_scale_table")
-        first_signs, second_signs, third_signs = [signs[:, n * PACK * V : (n + 1) * PACK * V] for n in range(3)]
+        sign_of = [signs[:, n * PACK * V : (n + 1) * PACK * V] for n in range(3)]
         for a in range(2):
             cols = slice(2 * a * V, 2 * (a + 1) * V)
-            nc.sync.dma_start(first_signs[:, cols], sign_rows[0][:, cols])
-        nc.sync.dma_start(second_signs, sign_rows[1])
-        nc.sync.dma_start(third_signs, sign_rows[2])
+            for n in range(2):
+                nc.sync.dma_start(sign_of[n][:, cols], sign_rows[n][:, cols])
+        nc.sync.dma_start(sign_of[2], sign_rows[2])
         w2_scale_spread = sb("w2_scale_spread", N, U8)
         nc.vector.tensor_copy(
             w2_scale_spread[:].rearrange("p (t c i) -> p c t i", t=PACK, i=16),
@@ -137,16 +136,15 @@ def tile_picked_csketch_silu_po_kernel(
                 engine_copy = nc.vector.tensor_copy if (t, a) == (0, 0) else nc.scalar.copy
                 engine_copy(y[t][:, cols], acc[:])
 
-        looked = [shared("looked0", PACK * V, F32, "w1_bf1"), sb("looked1", PACK * V, F32)]
-        second_plain = sb("second_plain", PACK * V, F32)
+        signed = shared("signed", 2 * PACK * V, F32, "w1_bf1")
+        looked = [signed[:, : PACK * V], signed[:, PACK * V :]]
+        plain = sb("plain", 2 * 2 * V, F32)
         third_plain = [sb("third_plain%d" % h, PACK * HALF, F32) for h in range(2)]
         third = [sb("third%d" % h, PACK * HALF, F32) for h in range(2)]
         hi = sb("hi", PACK * V, F32)
         lo = sb("lo", PACK * V, F32)
-        capped = [sb("capped%d" % h, PACK * HALF, F32) for h in range(2)]
         median = [shared("median%d" % h, PACK * HALF, F32, "median%d" % h) for h in range(2)]
         z_bf = [sb("z_bf%d" % h, PACK * HALF, BF16) for h in range(2)]
-        z_code = [sb("z_code%d" % h, HALF, U32) for h in range(2)]
         z_scale = [sb("z_scale%d" % h, HALF, U8) for h in range(2)]
         res_bf = [sb("res_bf%d" % h, PACK * HALF, BF16) for h in range(2)]
         res_code = sb("res_code", V, U32)
@@ -154,13 +152,21 @@ def tile_picked_csketch_silu_po_kernel(
         out_rows = out_0.rearrange("(p t) v -> p t v", t=PACK)
         out_words = out_1[0].rearrange("p c r -> p (c r)").bitcast(I32)
 
-        def look_signed(t):
+        def look_signed(n, t):
             cols = slice(t * V, (t + 1) * V)
-            nc.vector.tensor_tensor(looked[0][:, cols], y[t][:].indirect(hash_sb[0][:]), first_signs[:, cols], ALU.mult)
+            nc.vector.tensor_tensor(looked[n][:, cols], y[t][:].indirect(hash_sb[n][:]), sign_of[n][:, cols], ALU.mult)
 
-        def look_plain(out, n, t, k0, k1):
+        def look_plain(out, place, n, t, k0, k1):
             picked = y[t][:].indirect(hash_sb[n][:, k0 // 16 : k1 // 16])
-            nc.scalar.activation(out[:, t * (k1 - k0) : (t + 1) * (k1 - k0)], picked, COPY)
+            nc.scalar.activation(out[:, place * (k1 - k0) : (place + 1) * (k1 - k0)], picked, COPY)
+
+        def sign_both(t):
+            out, sign = [
+                tile[:, : 2 * PACK * V].rearrange("p (n t v) -> p n t v", n=2, t=PACK)[:, :, t, :]
+                for tile in (signed, signs)
+            ]
+            picked = plain[:, (t - 2) * 2 * V : (t - 1) * 2 * V].rearrange("p (n v) -> p n v", n=2)
+            nc.vector.tensor_tensor(out, picked, sign, ALU.mult)
 
         def keys(tile, k0, k1):
             return tile[:].rearrange("p (t v) -> p t v", t=PACK)[:, :, k0:k1]
@@ -170,16 +176,19 @@ def tile_picked_csketch_silu_po_kernel(
             nc.vector.tensor_tensor(out[:, cols], in0[:, cols], in1[:, cols], op)
 
         def sign_third(h):
-            sign = keys(third_signs, h * HALF, (h + 1) * HALF)
+            sign = keys(sign_of[2], h * HALF, (h + 1) * HALF)
             nc.vector.tensor_tensor(keys(third[h], 0, HALF), keys(third_plain[h], 0, HALF), sign, ALU.mult)
 
         def cap(h, k0, k1):
+            name = "capped%d_%d" % (h, k0)
+            capped = shared(name, PACK * (k1 - k0), F32, name)
             high = keys(hi, h * HALF + k0, h * HALF + k1)
-            nc.vector.tensor_tensor(keys(capped[h], k0, k1), high, keys(third[h], k0, k1), ALU.min)
+            nc.vector.tensor_tensor(keys(capped, 0, k1 - k0), high, keys(third[h], k0, k1), ALU.min)
+            return capped
 
-        def mid(h, k0, k1):
+        def mid(h, capped, k0, k1):
             low = keys(lo, h * HALF + k0, h * HALF + k1)
-            nc.vector.tensor_tensor(keys(median[h], k0, k1), low, keys(capped[h], k0, k1), ALU.max)
+            nc.vector.tensor_tensor(keys(median[h], k0, k1), low, keys(capped, 0, k1 - k0), ALU.max)
 
         def woven(tile):
             return tile[:].rearrange("p (c i t) -> p c t i", t=PACK, i=4)
@@ -221,38 +230,38 @@ def tile_picked_csketch_silu_po_kernel(
             cols = slice(h * HALF, (h + 1) * HALF)
             nc.vector.quantize_mx(out=res_code[:, cols].bitcast(FP8X4), scales=res_scale[:, cols], in_=res_bf[h][:])
 
-        for t in range(PACK):
-            look_signed(t)
-        for t in range(PACK):
-            look_plain(second_plain, 1, t, 0, V)
+        for n in range(2):
+            for t in range(2):
+                look_signed(n, t)
+        for t in range(2, PACK):
+            for n in range(2):
+                look_plain(plain, 2 * (t - 2) + n, n, t, 0, V)
         for h in range(2):
             for t in range(PACK):
-                look_plain(third_plain[h], 2, t, h * HALF, (h + 1) * HALF)
+                look_plain(third_plain[h], t, 2, t, h * HALF, (h + 1) * HALF)
         w2_word = sb("w2_word", N, U32)
         nc.scalar.copy(
             w2_word[:].rearrange("p (t c i) -> p c t i", t=PACK, i=4),
             w2_word_raw[:].bitcast(U32).rearrange("p (c i t) -> p c t i", t=PACK, i=4),
         )
-        on_planes(ALU.mult, looked[1], second_plain, second_signs, 0, 1)
-        on_planes(ALU.mult, looked[1], second_plain, second_signs, 1, 2)
-        on_planes(ALU.max, hi, looked[0], looked[1], 0, 1)
-        on_planes(ALU.mult, looked[1], second_plain, second_signs, 2, 3)
-        on_planes(ALU.min, lo, looked[0], looked[1], 0, 2)
-        on_planes(ALU.mult, looked[1], second_plain, second_signs, 3, 4)
+        on_planes(ALU.min, lo, looked[0], looked[1], 0, 1)
+        on_planes(ALU.max, hi, looked[0], looked[1], 0, 2)
+        sign_both(2)
+        on_planes(ALU.min, lo, looked[0], looked[1], 1, 2)
+        sign_both(3)
         on_planes(ALU.min, lo, looked[0], looked[1], 2, 3)
-        on_planes(ALU.max, hi, looked[0], looked[1], 1, 4)
+        on_planes(ALU.max, hi, looked[0], looked[1], 2, 4)
         sign_third(0)
         on_planes(ALU.min, lo, looked[0], looked[1], 3, 4)
-        cap(0, 0, HALF)
+        first_capped = cap(0, 0, HALF)
         sign_third(1)
-        mid(0, 0, HALF)
+        mid(0, first_capped, 0, HALF)
         silu(0, 0, HALF)
-        for k0 in (0, QUARTER):
-            cap(1, k0, k0 + QUARTER)
-        last_pieces = ((0, QUARTER), (QUARTER, QUARTER + EIGHTH), (QUARTER + EIGHTH, HALF))
-        for k0, k1 in last_pieces:
-            mid(1, k0, k1)
-            silu(1, k0, k1)
+        last_capped = [cap(1, k0, k0 + QUARTER) for k0 in (0, QUARTER)]
+        for capped, k0 in zip(last_capped, (0, QUARTER)):
+            mid(1, capped, k0, k0 + QUARTER)
+            silu(1, k0, k0 + QUARTER)
+        z_code = [shared("z_code0", HALF, U32, "capped1_0"), sb("z_code1", HALF, U32)]
         quantise_z(0, 0, HALF)
         first_high = second(0, 2, 4, "bank1")
         first_low = second(0, 0, 2, "bank0")

@@ -100,9 +100,9 @@ def tile_picked_csketch_silu_po_kernel(
         x_word = sb("x_word", S, U32)
         nc.vector.tensor_copy(x_word[:], x_word_table[:].bitcast(U32).indirect(offs_sb[:]))
 
-        for t in range(2):
-            nc.vector.tensor_copy(w1_dst[0][:, :80, t, 2:4], w1_src[1][:, :80, t, :])
-            nc.scalar.copy(w1_dst[0][:, 80:, t, 2:4], w1_src[1][:, 80:, t, :])
+        nc.vector.tensor_copy(w1_dst[0][:, :80, 0, 2:4], w1_src[1][:, :80, 0, :])
+        nc.scalar.copy(w1_dst[0][:, 80:, 0, 2:4], w1_src[1][:, 80:, 0, :])
+        nc.vector.tensor_copy(w1_dst[0][:, :, 1, 2:4], w1_src[1][:, :, 1, :])
         nc.scalar.copy(w1_dst[1][:, :, :, 2:4], w1_src[1][:, :, 2:4, :])
         w2_word_raw = shared("w2_word_raw", N, I32, "w1_raw1")
         nc.sync.dma_start(w2_word_raw[:], words(w2_words[0].rearrange("p c r -> p (c r)")))
@@ -128,13 +128,12 @@ def tile_picked_csketch_silu_po_kernel(
                 stop=True,
             )
 
-        for t in range(PACK):
-            for a in range(2):
-                cols = slice(a * S // 2, (a + 1) * S // 2)
-                acc = psum.tile([P, S // 2], F32, name="y_acc%d_%d" % (t, a), tag="bank%d" % (2 * t + a))
-                first(acc[:], t, cols)
-                engine_copy = nc.vector.tensor_copy if (t, a) == (0, 0) else nc.scalar.copy
-                engine_copy(y[t][:, cols], acc[:])
+        pieces = [(0, a * P, (a + 1) * P, bank) for a, bank in enumerate((6, 7, 0, 1))]
+        pieces.extend((t, a * S // 2, (a + 1) * S // 2, 2 * t + a) for t in range(1, PACK) for a in range(2))
+        for t, c0, c1, bank in pieces:
+            acc = psum.tile([P, c1 - c0], F32, name="y_acc%d_%d" % (t, c0), tag="bank%d" % bank)
+            first(acc[:], t, slice(c0, c1))
+            nc.scalar.copy(y[t][:, c0:c1], acc[:])
 
         signed = shared("signed", 2 * PACK * V, F32, "w1_bf1")
         looked = [signed[:, : PACK * V], signed[:, PACK * V :]]

@@ -229,8 +229,8 @@ def tile_picked_csketch_silu_po_kernel(
             cols = slice(h * HALF, (h + 1) * HALF)
             nc.vector.quantize_mx(out=res_code[:, cols].bitcast(FP8X4), scales=res_scale[:, cols], in_=res_bf[h][:])
 
-        for n in range(2):
-            for t in range(2):
+        for t in range(2):
+            for n in range(2):
                 look_signed(n, t)
         for t in range(2, PACK):
             for n in range(2):

@@ -46,7 +46,7 @@ def tile_picked_csketch_silu_po_kernel(
 
         def place_scale_rows(plane_tile, spread_tile):
             for r in range(QUADS):
-                nc.sync.dma_start(words(plane_tile[r:P:32, :]), words(spread_tile[8 * r : P : 32, :]))
+                nc.sync.dma_start(words(plane_tile[r:P:32, :]), words(spread_tile[32 + 4 * r : 96 : 16, :]))
 
         x_scale_table = shared("x_scale_table", T, U8, "x_scale_table")
         w2_scale_raw = sb("w2_scale_raw", N, U8)
@@ -63,8 +63,8 @@ def tile_picked_csketch_silu_po_kernel(
         w1_raw = [shared("w1_raw%d" % b, 2 * H, F32, "w1_raw%d" % b) for b in range(2)]
         nc.sync.dma_start(w1_raw[0][:], w1_rows[:, : 2 * H])
         nc.sync.dma_start(offs_sb[:], offs)
-        nc.sync.dma_start(words(x_scale_table[0:P:8, :]), words(x_scales[0]))
-        nc.sync.dma_start(words(w2_scale_raw[0:P:8, :]), words(w2_scales[0]))
+        nc.sync.dma_start(words(x_scale_table[32:96:4, :]), words(x_scales[0]))
+        nc.sync.dma_start(words(w2_scale_raw[32:96:4, :]), words(w2_scales[0]))
         x_word_table = shared("x_word_table", T, I32, "x_word_table")
         nc.sync.dma_start(x_word_table[:], words(x_words[0].rearrange("p c r -> p (c r)")))
         nc.sync.dma_start(hash_sb[0][:], h1)
@@ -277,8 +277,8 @@ def tile_picked_csketch_silu_po_kernel(
         nc.vector.tensor_copy(woven(res_bf[0]), planes(first_res[:], PACK))
         nc.scalar.copy(last_res[:, low], last_low[:])
         store_rows(nc.sync, last_res, 0, 2, 1)
-        quantise_res(0)
         nc.vector.tensor_copy(woven(res_bf[1])[:, :, 0:2], planes(last_res[:, low], 2))
+        quantise_res(0)
         nc.scalar.copy(woven(res_bf[1])[:, :, 2:4], planes(last_high[:], 2))
         nc.scalar.copy(last_res[:, high], last_high[:])
         store_rows(nc.scalar, last_res, 2, PACK, 1)

@@ -148,7 +148,6 @@ def tile_picked_csketch_silu_po_kernel(
         res_bf = [sb("res_bf%d" % h, PACK * HALF, BF16) for h in range(2)]
         res_code = sb("res_code", V, U32)
         res_scale = sb("res_scale", V, U8)
-        out_rows = out_0.rearrange("(p t) v -> p t v", t=PACK)
         out_words = out_1[0].rearrange("p c r -> p (c r)").bitcast(I32)
 
         def look_signed(n, t):
@@ -221,10 +220,6 @@ def tile_picked_csketch_silu_po_kernel(
                 )
             return acc
 
-        def store_rows(queue, res, t0, t1, h):
-            rows = res[:, t0 * HALF : t1 * HALF].rearrange("p (t v) -> p t v", v=HALF)
-            queue.dma_start(out_rows[:, t0:t1, h * HALF : (h + 1) * HALF], rows)
-
         def quantise_res(h):
             cols = slice(h * HALF, (h + 1) * HALF)
             nc.vector.quantize_mx(out=res_code[:, cols].bitcast(FP8X4), scales=res_scale[:, cols], in_=res_bf[h][:])
@@ -268,20 +263,31 @@ def tile_picked_csketch_silu_po_kernel(
         quantise_z(1, QUARTER, HALF)
         last_low = second(1, 0, 2, "bank2")
         last_high = second(1, 2, 4, "bank3")
-        first_res = shared("first_res", PACK * HALF, F32, "median1")
-        last_res = sb("last_res", PACK * HALF, F32)
-        low, high = slice(0, 2 * HALF), slice(2 * HALF, PACK * HALF)
-        nc.vector.tensor_copy(first_res[:, low], first_low[:])
-        nc.scalar.copy(first_res[:, high], first_high[:])
-        store_rows(nc.sync, first_res, 0, PACK, 0)
-        nc.vector.tensor_copy(woven(res_bf[0]), planes(first_res[:], PACK))
-        nc.scalar.copy(last_res[:, low], last_low[:])
-        store_rows(nc.sync, last_res, 0, 2, 1)
-        nc.vector.tensor_copy(woven(res_bf[1])[:, :, 0:2], planes(last_res[:, low], 2))
+        res = shared("res", PACK * V, F32, "median1")
+        res_low, res_high = res[:, : 2 * V], res[:, 2 * V :]
+
+        def pair(tile, h):
+            return tile.rearrange("p (t v) -> p t v", v=V)[:, :, h * HALF : (h + 1) * HALF]
+
+        def pair_planes(tile, h):
+            return pair(tile, h).rearrange("p t (c i) -> p c t i", i=4)
+
+        def bank_pair(acc):
+            return acc[:].rearrange("p (t v) -> p t v", t=2)
+
+        out_pairs = out_0.rearrange("(p a t) v -> p a (t v)", a=2, t=2)
+        out_rows = out_0.rearrange("(p t) v -> p t v", t=PACK)
+        nc.vector.tensor_copy(pair(res_low, 0), bank_pair(first_low))
+        nc.scalar.copy(pair(res_high, 0), bank_pair(first_high))
+        nc.sync.dma_start(out_rows[:, 2:4, :HALF], pair(res_high, 0))
+        nc.vector.tensor_copy(woven(res_bf[0]), pair_planes(res[:], 0))
+        nc.scalar.copy(pair(res_low, 1), bank_pair(last_low))
+        nc.sync.dma_start(out_pairs[:, 0, :], res_low)
+        nc.vector.tensor_copy(woven(res_bf[1])[:, :, 0:2], pair_planes(res_low, 1))
         quantise_res(0)
         nc.scalar.copy(woven(res_bf[1])[:, :, 2:4], planes(last_high[:], 2))
-        nc.scalar.copy(last_res[:, high], last_high[:])
-        store_rows(nc.scalar, last_res, 2, PACK, 1)
+        nc.scalar.copy(pair(res_high, 1), bank_pair(last_high))
+        nc.scalar.dma_start(out_rows[:, 2:4, HALF:], pair(res_high, 1))
         quantise_res(1)
         nc.sync.dma_start(out_words, res_code[:].bitcast(I32))
         for q in range(QUADS):

@@ -45,14 +45,14 @@ def tile_picked_csketch_silu_po_kernel(
             return keep.tile([P, cols], dtype, name=name, tag=tag, align_bytes=64)
 
         def place_scale_rows(plane_tile, spread_tile):
-            for r in range(QUADS):
-                nc.sync.dma_start(words(plane_tile[r:P:32, :]), words(spread_tile[32 + 4 * r : 96 : 16, :]))
+            for r in range(1, QUADS):
+                nc.sync.dma_start(words(plane_tile[r:P:32, :]), words(spread_tile[8 * r : P : 32, :]))
 
         x_scale_table = shared("x_scale_table", T, U8, "x_scale_table")
         w2_scale_raw = sb("w2_scale_raw", N, U8)
         x_scale = sb("x_scale", S, U8)
         w2_scale = sb("w2_scale", N, U8)
-        for tile in (x_scale_table, w2_scale_raw, x_scale, w2_scale):
+        for tile in (x_scale_table, w2_scale_raw):
             nc.vector.memset(words(tile[:]), 0)
         warm_in = sb("warm_in", 8, F32)
         warm_out = sb("warm_out", 8, F32)
@@ -63,18 +63,18 @@ def tile_picked_csketch_silu_po_kernel(
         w1_raw = [shared("w1_raw%d" % b, 2 * H, F32, "w1_raw%d" % b) for b in range(2)]
         nc.sync.dma_start(w1_raw[0][:], w1_rows[:, : 2 * H])
         nc.sync.dma_start(offs_sb[:], offs)
-        nc.sync.dma_start(words(x_scale_table[32:96:4, :]), words(x_scales[0]))
-        nc.sync.dma_start(words(w2_scale_raw[32:96:4, :]), words(w2_scales[0]))
+        nc.sync.dma_start(words(x_scale_table[0:P:8, :]), words(x_scales[0]))
+        nc.sync.dma_start(words(w2_scale_raw[0:P:8, :]), words(w2_scales[0]))
         x_word_table = shared("x_word_table", T, I32, "x_word_table")
         nc.sync.dma_start(x_word_table[:], words(x_words[0].rearrange("p c r -> p (c r)")))
-        nc.sync.dma_start(hash_sb[0][:], h1)
         nc.sync.dma_start(w1_raw[1][:], w1_rows[:, 2 * H :])
-        for tile, h in zip(hash_sb[1:], (h2, h3)):
+        for tile, h in zip(hash_sb, (h1, h2, h3)):
             nc.sync.dma_start(tile[:], h)
         sign_rows = [sg.rearrange("(p t) v -> p (t v)", t=PACK) for sg in (sg1, sg2, sg3)]
 
         x_scale_spread = sb("x_scale_spread", S, U8)
         nc.vector.tensor_copy(x_scale_spread[:], x_scale_table[:].indirect(offs_sb[:]))
+        nc.vector.tensor_copy(words(x_scale[:]), words(x_scale_spread[:]))
         place_scale_rows(x_scale, x_scale_spread)
         signs = shared("signs", 3 * PACK * V, F32, "x_scale_table")
         sign_of = [signs[:, n * PACK * V : (n + 1) * PACK * V] for n in range(3)]
@@ -83,9 +83,8 @@ def tile_picked_csketch_silu_po_kernel(
             for n in range(2):
                 nc.sync.dma_start(sign_of[n][:, cols], sign_rows[n][:, cols])
         nc.sync.dma_start(sign_of[2], sign_rows[2])
-        w2_scale_spread = sb("w2_scale_spread", N, U8)
         nc.vector.tensor_copy(
-            w2_scale_spread[:].rearrange("p (t c i) -> p c t i", t=PACK, i=16),
+            w2_scale[:].rearrange("p (t c i) -> p c t i", t=PACK, i=16),
             w2_scale_raw[:].rearrange("p (c i t) -> p c t i", t=PACK, i=16),
         )
 
@@ -96,7 +95,7 @@ def tile_picked_csketch_silu_po_kernel(
         w1_dst = [tile[:].rearrange("p (t m j) -> p m t j", t=2, j=PACK) for tile in w1_bf]
         nc.scalar.copy(w1_dst[0][:, :, :, 0:2], w1_src[0][:, :, 0:2, :])
         nc.scalar.copy(w1_dst[1][:, :, :, 0:2], w1_src[0][:, :, 2:4, :])
-        place_scale_rows(w2_scale, w2_scale_spread)
+        place_scale_rows(w2_scale, w2_scale)
         x_word = sb("x_word", S, U32)
         nc.vector.tensor_copy(x_word[:], x_word_table[:].bitcast(U32).indirect(offs_sb[:]))
 

from contextlib import ExitStack

import concourse.mybir as mybir

K, T, S, V, N, H = 512, 2048, 512, 256, 512, 512
FLOPS = 2 * K * H * S + 2 * H * N * V

F32 = mybir.dt.float32
BF16 = mybir.dt.bfloat16
I32 = mybir.dt.int32
U32 = mybir.dt.uint32
U16 = mybir.dt.uint16
U8 = mybir.dt.uint8
FP8X4 = mybir.dt.float8_e4m3fn_x4
ALU = mybir.AluOpType
SILU = mybir.ActivationFunctionType.Silu
COPY = mybir.ActivationFunctionType.Copy

P = 128
PACK = 4
QUADS = 4
HALF = V // 2
QUARTER = V // 4


def tile_picked_csketch_silu_po_kernel(
    tc, x_words, x_scales, w1, sg1, sg2, sg3, w2_words, w2_scales, offs, h1, h2, h3, out_0, out_1, out_2
):
    nc = tc.nc
    with ExitStack() as ctx:
        lists = ctx.enter_context(tc.tile_pool(name="lists", bufs=1))
        keep = ctx.enter_context(tc.tile_pool(name="keep", bufs=1))
        psum = ctx.enter_context(tc.psum_pool(name="psum", bufs=1))

        def sb(name, cols, dtype):
            return keep.tile([P, cols], dtype, name=name, align_bytes=64)

        offs_sb = lists.tile([P, S // 16], U16, name="offs_sb")
        hash_sb = [lists.tile([P, V // 16], U16, name="hash%d" % n) for n in range(3)]

        def words(ap):
            return ap.bitcast(I32)

        def shared(name, cols, dtype, tag):
            return keep.tile([P, cols], dtype, name=name, tag=tag, align_bytes=64)

        def place_scale_rows(plane_tile, spread_tile):
            for r in range(1, QUADS):
                nc.sync.dma_start(words(plane_tile[r:P:32, :]), words(spread_tile[8 * r : P : 32, :]))

        x_scale_table = shared("x_scale_table", T, U8, "x_scale_table")
        w2_scale_raw = sb("w2_scale_raw", N, U8)
        x_scale = sb("x_scale", S, U8)
        w2_scale = sb("w2_scale", N, U8)
        for tile in (x_scale_table, w2_scale_raw):
            nc.vector.memset(words(tile[:]), 0)
        warm_in = sb("warm_in", 8, F32)
        warm_out = sb("warm_out", 8, F32)
        nc.vector.memset(warm_in[:], 0.0)
        nc.scalar.activation(warm_out[:], warm_in[:], SILU)

        w1_rows = w1.rearrange("(p j) c -> p (j c)", j=PACK)
        w1_raw = [shared("w1_raw%d" % b, 2 * H, F32, "w1_raw%d" % b) for b in range(2)]
        nc.sync.dma_start(w1_raw[0][:], w1_rows[:, : 2 * H])
        nc.sync.dma_start(offs_sb[:], offs)
        nc.sync.dma_start(words(x_scale_table[0:P:8, :]), words(x_scales[0]))
        nc.sync.dma_start(words(w2_scale_raw[0:P:8, :]), words(w2_scales[0]))
        x_word_table = shared("x_word_table", T, I32, "x_word_table")
        nc.sync.dma_start(x_word_table[:], words(x_words[0].rearrange("p c r -> p (c r)")))
        nc.sync.dma_start(w1_raw[1][:], w1_rows[:, 2 * H :])
        for tile, h in zip(hash_sb, (h1, h2, h3)):
            nc.sync.dma_start(tile[:], h)
        sign_rows = [sg.rearrange("(p t) v -> p (t v)", t=PACK) for sg in (sg1, sg2, sg3)]

        x_scale_spread = sb("x_scale_spread", S, U8)
        nc.vector.tensor_copy(x_scale_spread[:], x_scale_table[:].indirect(offs_sb[:]))
        nc.vector.tensor_copy(words(x_scale[:]), words(x_scale_spread[:]))
        place_scale_rows(x_scale, x_scale_spread)
        signs = shared("signs", 3 * PACK * V, F32, "x_scale_table")
        sign_of = [signs[:, n * PACK * V : (n + 1) * PACK * V] for n in range(3)]
        for a in range(2):
            cols = slice(2 * a * V, 2 * (a + 1) * V)
            for n in range(2):
                nc.sync.dma_start(sign_of[n][:, cols], sign_rows[n][:, cols])
        nc.sync.dma_start(sign_of[2], sign_rows[2])
        nc.vector.tensor_copy(
            w2_scale[:].rearrange("p (t c i) -> p c t i", t=PACK, i=16),
            w2_scale_raw[:].rearrange("p (c i t) -> p c t i", t=PACK, i=16),
        )

        w1_src = [tile[:].rearrange("p (j m t) -> p m t j", t=PACK, j=2) for tile in w1_raw]
        w1_bf = [shared("w1_bf%d" % a, 2 * H, BF16, "w1_bf%d" % a) for a in range(2)]
        w1_code = [sb("w1_code0", 2 * P, U32)]
        w1_scale = [sb("w1_scale%d" % a, 2 * P, U8) for a in range(2)]
        w1_dst = [tile[:].rearrange("p (t m j) -> p m t j", t=2, j=PACK) for tile in w1_bf]
        nc.scalar.copy(w1_dst[0][:, :, :, 0:2], w1_src[0][:, :, 0:2, :])
        nc.scalar.copy(w1_dst[1][:, :, :, 0:2], w1_src[0][:, :, 2:4, :])
        place_scale_rows(w2_scale, w2_scale)
        x_word = sb("x_word", S, U32)
        nc.vector.tensor_copy(x_word[:], x_word_table[:].bitcast(U32).indirect(offs_sb[:]))

        nc.vector.tensor_copy(w1_dst[0][:, :80, 0, 2:4], w1_src[1][:, :80, 0, :])
        nc.scalar.copy(w1_dst[0][:, 80:, 0, 2:4], w1_src[1][:, 80:, 0, :])
        nc.vector.tensor_copy(w1_dst[0][:, :, 1, 2:4], w1_src[1][:, :, 1, :])
        nc.scalar.copy(w1_dst[1][:, :, :, 2:4], w1_src[1][:, :, 2:4, :])
        w2_word_raw = shared("w2_word_raw", N, I32, "w1_raw1")
        nc.sync.dma_start(w2_word_raw[:], words(w2_words[0].rearrange("p c r -> p (c r)")))
        for t in range(2):
            nc.vector.quantize_mx(
                out=w1_code[0][:, t * P : (t + 1) * P].bitcast(FP8X4),
                scales=w1_scale[0][:, t * P : (t + 1) * P],
                in_=w1_bf[0][:, t * H : (t + 1) * H],
            )
        w1_code.append(sb("w1_code1", 2 * P, U32))
        nc.vector.quantize_mx(out=w1_code[1][:].bitcast(FP8X4), scales=w1_scale[1][:], in_=w1_bf[1][:])
        y = [shared("y%d" % t, S, F32, "y%d" % t) for t in range(PACK)]

        def first(acc, t, cols):
            rows = slice(t % 2 * P, (t % 2 + 1) * P)
            nc.tensor.matmul_mx(
                out=acc,
                lhsT=w1_code[t // 2][:, rows].bitcast(FP8X4),
                lhsT_scale=w1_scale[t // 2][:, rows],
                rhs=x_word[:, cols].bitcast(FP8X4),
                rhs_scale=x_scale[:, cols],
                start=True,
                stop=True,
            )

        pieces = [(0, a * P, (a + 1) * P, bank) for a, bank in enumerate((6, 7, 0, 1))]
        pieces.extend((t, a * S // 2, (a + 1) * S // 2, 2 * t + a) for t in range(1, PACK) for a in range(2))
        for t, c0, c1, bank in pieces:
            acc = psum.tile([P, c1 - c0], F32, name="y_acc%d_%d" % (t, c0), tag="bank%d" % bank)
            first(acc[:], t, slice(c0, c1))
            nc.scalar.copy(y[t][:, c0:c1], acc[:])

        signed = shared("signed", 2 * PACK * V, F32, "w1_bf1")
        looked = [signed[:, : PACK * V], signed[:, PACK * V :]]
        plain = sb("plain", 2 * 2 * V, F32)
        third_plain = [sb("third_plain%d" % h, PACK * HALF, F32) for h in range(2)]
        third = [sb("third%d" % h, PACK * HALF, F32) for h in range(2)]
        hi = sb("hi", PACK * V, F32)
        lo = sb("lo", PACK * V, F32)
        median = [shared("median%d" % h, PACK * HALF, F32, "median%d" % h) for h in range(2)]
        z_bf = [sb("z_bf%d" % h, PACK * HALF, BF16) for h in range(2)]
        z_scale = [sb("z_scale%d" % h, HALF, U8) for h in range(2)]
        res_bf = [sb("res_bf%d" % h, PACK * HALF, BF16) for h in range(2)]
        res_code = sb("res_code", V, U32)
        res_scale = sb("res_scale", V, U8)
        out_words = out_1[0].rearrange("p c r -> p (c r)").bitcast(I32)

        def look_signed(n, t):
            cols = slice(t * V, (t + 1) * V)
            nc.vector.tensor_tensor(looked[n][:, cols], y[t][:].indirect(hash_sb[n][:]), sign_of[n][:, cols], ALU.mult)

        def look_plain(out, place, n, t, k0, k1):
            picked = y[t][:].indirect(hash_sb[n][:, k0 // 16 : k1 // 16])
            nc.scalar.activation(out[:, place * (k1 - k0) : (place + 1) * (k1 - k0)], picked, COPY)

        def sign_both(t):
            out, sign = [
                tile[:, : 2 * PACK * V].rearrange("p (n t v) -> p n t v", n=2, t=PACK)[:, :, t, :]
                for tile in (signed, signs)
            ]
            picked = plain[:, (t - 2) * 2 * V : (t - 1) * 2 * V].rearrange("p (n v) -> p n v", n=2)
            nc.vector.tensor_tensor(out, picked, sign, ALU.mult)

        def keys(tile, k0, k1):
            return tile[:].rearrange("p (t v) -> p t v", t=PACK)[:, :, k0:k1]

        def on_planes(op, out, in0, in1, t0, t1):
            cols = slice(t0 * V, t1 * V)
            nc.vector.tensor_tensor(out[:, cols], in0[:, cols], in1[:, cols], op)

        def sign_third(h):
            sign = keys(sign_of[2], h * HALF, (h + 1) * HALF)
            nc.vector.tensor_tensor(keys(third[h], 0, HALF), keys(third_plain[h], 0, HALF), sign, ALU.mult)

        def cap(h, k0, k1):
            name = "capped%d_%d" % (h, k0)
            capped = shared(name, PACK * (k1 - k0), F32, name)
            high = keys(hi, h * HALF + k0, h * HALF + k1)
            nc.vector.tensor_tensor(keys(capped, 0, k1 - k0), high, keys(third[h], k0, k1), ALU.min)
            return capped

        def mid(h, capped, k0, k1):
            low = keys(lo, h * HALF + k0, h * HALF + k1)
            nc.vector.tensor_tensor(keys(median[h], k0, k1), low, keys(capped, 0, k1 - k0), ALU.max)

        def woven(tile):
            return tile[:].rearrange("p (c i t) -> p c t i", t=PACK, i=4)

        def planes(ap, count):
            return ap.rearrange("p (t c i) -> p c t i", t=count, i=4)

        def silu(h, k0, k1):
            groups = slice(k0 // 4, k1 // 4)
            nc.scalar.activation(woven(z_bf[h])[:, groups], planes(median[h][:], PACK)[:, groups], SILU)

        def quantise_z(h, k0, k1):
            nc.vector.quantize_mx(
                out=z_code[h][:, k0:k1].bitcast(FP8X4),
                scales=z_scale[h][:, k0:k1],
                in_=z_bf[h][:, PACK * k0 : PACK * k1],
            )

        def second(h, t0, t1, tag):
            acc = psum.tile([P, (t1 - t0) * HALF], F32, name="out_acc%d_%d" % (h, t0), tag=tag)
            for t in range(t0, t1):
                rows = slice(t * P, (t + 1) * P)
                nc.tensor.matmul_mx(
                    out=acc[:, (t - t0) * HALF : (t - t0 + 1) * HALF],
                    lhsT=w2_word[:, rows].bitcast(FP8X4),
                    lhsT_scale=w2_scale[:, rows],
                    rhs=z_code[h][:].bitcast(FP8X4),
                    rhs_scale=z_scale[h][:],
                    start=True,
                    stop=True,
                )
            return acc

        def quantise_res(h):
            cols = slice(h * HALF, (h + 1) * HALF)
            nc.vector.quantize_mx(out=res_code[:, cols].bitcast(FP8X4), scales=res_scale[:, cols], in_=res_bf[h][:])

        for t in range(2):
            for n in range(2):
                look_signed(n, t)
        for t in range(2, PACK):
            for n in range(2):
                look_plain(plain, 2 * (t - 2) + n, n, t, 0, V)
        for h in range(2):
            for t in range(PACK):
                look_plain(third_plain[h], t, 2, t, h * HALF, (h + 1) * HALF)
        w2_word = sb("w2_word", N, U32)
        nc.scalar.copy(
            w2_word[:].rearrange("p (t c i) -> p c t i", t=PACK, i=4),
            w2_word_raw[:].bitcast(U32).rearrange("p (c i t) -> p c t i", t=PACK, i=4),
        )
        on_planes(ALU.min, lo, looked[0], looked[1], 0, 1)
        on_planes(ALU.max, hi, looked[0], looked[1], 0, 2)
        sign_both(2)
        on_planes(ALU.min, lo, looked[0], looked[1], 1, 2)
        sign_both(3)
        on_planes(ALU.min, lo, looked[0], looked[1], 2, 3)
        on_planes(ALU.max, hi, looked[0], looked[1], 2, 4)
        sign_third(0)
        on_planes(ALU.min, lo, looked[0], looked[1], 3, 4)
        first_capped = cap(0, 0, HALF)
        sign_third(1)
        mid(0, first_capped, 0, HALF)
        silu(0, 0, HALF)
        last_capped = [cap(1, k0, k0 + QUARTER) for k0 in (0, QUARTER)]
        for capped, k0 in zip(last_capped, (0, QUARTER)):
            mid(1, capped, k0, k0 + QUARTER)
            silu(1, k0, k0 + QUARTER)
        z_code = [shared("z_code0", HALF, U32, "capped1_0"), sb("z_code1", HALF, U32)]
        quantise_z(0, 0, HALF)
        first_high = second(0, 2, 4, "bank1")
        first_low = second(0, 0, 2, "bank0")
        quantise_z(1, 0, QUARTER)
        quantise_z(1, QUARTER, HALF)
        last_low = second(1, 0, 2, "bank2")
        last_high = second(1, 2, 4, "bank3")
        res = shared("res", PACK * V, F32, "median1")
        res_low, res_high = res[:, : 2 * V], res[:, 2 * V :]

        def pair(tile, h):
            return tile.rearrange("p (t v) -> p t v", v=V)[:, :, h * HALF : (h + 1) * HALF]

        def pair_planes(tile, h):
            return pair(tile, h).rearrange("p t (c i) -> p c t i", i=4)

        def bank_pair(acc):
            return acc[:].rearrange("p (t v) -> p t v", t=2)

        out_pairs = out_0.rearrange("(p a t) v -> p a (t v)", a=2, t=2)
        out_rows = out_0.rearrange("(p t) v -> p t v", t=PACK)
        nc.vector.tensor_copy(pair(res_low, 0), bank_pair(first_low))
        nc.scalar.copy(pair(res_high, 0), bank_pair(first_high))
        nc.sync.dma_start(out_rows[:, 2:4, :HALF], pair(res_high, 0))
        nc.vector.tensor_copy(woven(res_bf[0]), pair_planes(res[:], 0))
        nc.scalar.copy(pair(res_low, 1), bank_pair(last_low))
        nc.sync.dma_start(out_pairs[:, 0, :], res_low)
        nc.vector.tensor_copy(woven(res_bf[1])[:, :, 0:2], pair_planes(res_low, 1))
        quantise_res(0)
        nc.scalar.copy(woven(res_bf[1])[:, :, 2:4], planes(last_high[:], 2))
        nc.scalar.copy(pair(res_high, 1), bank_pair(last_high))
        nc.scalar.dma_start(out_rows[:, 2:4, HALF:], pair(res_high, 1))
        quantise_res(1)
        nc.sync.dma_start(out_words, res_code[:].bitcast(I32))
        for q in range(QUADS):
            queue = nc.sync if q < 2 else nc.scalar
            queue.dma_start(
                out_2[0, q:16:4, :].bitcast(I32), res_scale[q:P:32, :].bitcast(I32)
            )
